import numpy as np
import ml_dtypes


def mxq(x, axis, fmt="e4m3"):
    dtype, down = {"e4m3": (ml_dtypes.float8_e4m3fn, 7), "e5m2": (ml_dtypes.float8_e5m2, 14)}[fmt]
    v = np.moveaxis(np.asarray(x, np.float32).astype(ml_dtypes.bfloat16).astype(np.float64), axis, -1)
    blocks = v.reshape(v.shape[:-1] + (-1, 32))
    amax = np.abs(blocks).max(-1, keepdims=True)
    byte = np.maximum(np.where(amax > 0, np.frexp(amax)[1] - 1 + 127, 0) - down, 1)
    scale = np.exp2(byte - 127.0)
    codes = (blocks / scale).astype(np.float32).astype(dtype).astype(np.float64)
    return np.moveaxis((codes * scale).reshape(v.shape), -1, axis)


WIDE = False


def mx_kscale(k):
    if not WIDE:
        return np.ones(k)
    levels = np.array([10, -10, 5, -5, 0])
    if k % 512:
        return np.exp2(np.random.permutation(np.resize(levels, k // 32))).repeat(32)
    a = np.empty((k // 512, 16))
    for p in range(k // 512):
        a[p, :8] = np.random.permutation(np.resize(levels, 8))
        for g in range(8):
            far = levels[np.abs(levels - a[p, g]) >= 10]
            a[p, g + 8] = far[np.random.randint(len(far))]
    return np.exp2(a.ravel()).repeat(32)


def f64(x):
    return np.asarray(x).astype(np.float64)


def striped(idx):
    return np.tile(idx.reshape(-1, 16).T, (8, 1)).astype(np.uint16)


def unstriped(offs):
    return offs[:16].T.reshape(-1).astype(np.int64)


def striped8(idx):
    return np.concatenate([x.reshape(-1, 16).T for x in idx]).astype(np.uint16)


def runs(offs, k):
    lists = np.stack([offs[16 * r : 16 * r + 16].T.reshape(-1) for r in range(8)]).astype(np.int64)
    return lists[np.arange(k) % 512 // 64]


def pack_weight(w):
    k, n = w.shape
    w = f64(np.asarray(w, np.float32).astype(ml_dtypes.bfloat16)).reshape(k // 32, 32, n)
    amax = np.abs(w).max(1)
    byte = np.clip(np.where(amax > 0, np.frexp(amax)[1] - 1 + 127 - 7, 1), 1, 254)
    scaled = (w * np.exp2(127.0 - byte)[:, None, :]).reshape(k, n).astype(np.float32)
    words = np.ascontiguousarray(scaled.reshape(k // 512, 128, 4, n).transpose(0, 1, 3, 2)).astype(ml_dtypes.float8_e4m3fn).view(np.uint8)
    return words, np.ascontiguousarray(byte.astype(np.uint8).reshape(k // 512, 16, n))


def unpack_weight(words, scales):
    g, p, n, _ = words.shape
    vals = np.ascontiguousarray(words).view(ml_dtypes.float8_e4m3fn).astype(np.float64) * np.repeat(np.exp2(scales.astype(np.float64) - 127.0), 8, axis=1)[..., None]
    return vals.transpose(0, 1, 3, 2).reshape(g * 512, n)


K, T, S, N, U, H = 512, 2048, 512, 512, 1024, 512


def setup_inputs():
    n = np.random.standard_normal
    s = mx_kscale(K)[:, None]
    u = mx_kscale(H)
    packed_xT = pack_weight(n((K, T)) * s)
    return {
        "x_words": packed_xT[0],
        "x_scales": packed_xT[1],
        "w1": (n((K, H)) / np.sqrt(K) / s * u).astype(np.float32),
        "mem": (n((H, U)) * u[:, None]).astype(np.float32),
        "w2": (n((H, N)) / np.sqrt(H) / u[:, None]).astype(np.float32),
        "offs": striped(np.random.permutation(T)[:S]),
        "slot": striped8(np.stack([np.random.permutation(U)[:S] for _ in range(8)])),
    }


def reference(x_words, x_scales, w1, mem, w2, offs, slot):
    xq = unpack_weight(x_words, x_scales)[:, unstriped(offs)]
    y = mxq(f64(w1), 0, "e4m3").T @ xq
    z = f64(mem).copy()
    z[np.arange(H)[:, None], runs(slot, H)] = y
    return mxq(f64(w2), 0, "e4m3").T @ mxq(z, 0, "e4m3")

@@ -1,0 +1,150 @@
+from contextlib import ExitStack
+
+import concourse.mybir as mybir
+
+K, T, S, H, U, N = 512, 2048, 512, 512, 1024, 512
+FLOPS = 2 * K * H * S + 2 * H * N * U
+
+F32 = mybir.dt.float32
+BF16 = mybir.dt.bfloat16
+I32 = mybir.dt.int32
+U32 = mybir.dt.uint32
+U16 = mybir.dt.uint16
+U8 = mybir.dt.uint8
+FP8X4 = mybir.dt.float8_e4m3fn_x4
+
+P = 128
+PACK = 4
+BANK = 512
+HALF = S // 2
+CHUNKS = (128, 128, 256, 256, 256)
+VECTOR_BANKS = 2
+
+
+def tile_picked_pagemix_none_p_kernel(tc, x_words, x_scales, w1, mem, w2, offs, slot, out):
+    nc = tc.nc
+    with ExitStack() as ctx:
+        keep = ctx.enter_context(tc.tile_pool(name="keep", bufs=1))
+        psum = ctx.enter_context(tc.psum_pool(name="psum", bufs=8))
+
+        offs_sb = keep.tile([P, S // 16], U16, name="offs_sb")
+        slot_sb = keep.tile([P, S // 16], U16, name="slot_sb")
+        xw = keep.tile([P, T], U32, name="xw", align_bytes=64)
+        xs = keep.tile([P, T], U8, name="xs", align_bytes=64)
+        w1_raw = keep.tile([P, PACK, H], F32, name="w1_raw", align_bytes=64)
+        w2_raw = keep.tile([P, PACK, N], F32, name="w2_raw", align_bytes=64)
+        page3 = keep.tile([P, U], F32, name="page3", align_bytes=64)
+        page1 = keep.tile([P, U], F32, name="page1", align_bytes=64)
+        page23 = keep.tile([P, 2 * U], F32, name="page23", align_bytes=64)
+        page01 = keep.tile([P, 2 * U], F32, name="page01", align_bytes=64)
+
+        mem_rows = mem.rearrange("(p t) w -> t p w", t=PACK)
+        nc.vector.memset(xs[:].bitcast(I32), 0)
+        nc.sync.dma_start(offs_sb[:], offs)
+        nc.sync.dma_start(w1_raw[:], w1.rearrange("(p j) c -> p j c", j=PACK))
+        scale_rows = x_scales[0].rearrange("(q r) c -> r q c", r=4)
+        for r in range(4):
+            nc.scalar.dma_start(xs[r:P:32, :].bitcast(I32), scale_rows[r].bitcast(I32))
+        nc.sync.dma_start(xw[:].bitcast(I32), x_words[0].rearrange("p c r -> p (c r)").bitcast(I32))
+        nc.sync.dma_start(slot_sb[:], slot)
+        nc.sync.dma_start(page3[:], mem_rows[3])
+        nc.sync.dma_start(page1[:], mem_rows[1])
+        nc.sync.dma_start(w2_raw[:], w2.rearrange("(p j) c -> p j c", j=PACK))
+        nc.sync.dma_start(page23[:, 0:U], mem_rows[2])
+        nc.sync.dma_start(page01[:, 0:U], mem_rows[0])
+
+        gs = keep.tile([P, S], U8, name="gs", align_bytes=64)
+        for h in range(2):
+            nc.vector.tensor_copy(gs[:, h * HALF:(h + 1) * HALF], xs[:].indirect(offs_sb[:, h * 16:(h + 1) * 16]))
+
+        w1_src = w1_raw[:].rearrange("p j (m t) -> p m j t", t=PACK)
+        w1_codes = {}
+        w1_scales = {}
+        for t0, copy in ((2, nc.vector.tensor_copy), (0, nc.scalar.copy)):
+            grouped = keep.tile([P, 2, P, PACK], BF16, name="w1_grouped%d" % t0, align_bytes=64)
+            copy(grouped[:].rearrange("p t m j -> p m j t"), w1_src[:, :, :, t0:t0 + 2])
+            codes = keep.tile([P, 2 * P], U32, name="w1_codes%d" % t0, align_bytes=64)
+            scales = keep.tile([P, 2 * P], U8, name="w1_scales%d" % t0, align_bytes=64)
+            nc.vector.quantize_mx(out=codes[:].bitcast(FP8X4), scales=scales[:], in_=grouped[:].rearrange("p t m j -> p (t m j)"))
+            for i in range(2):
+                w1_codes[t0 + i] = codes[:, i * P:(i + 1) * P]
+                w1_scales[t0 + i] = scales[:, i * P:(i + 1) * P]
+
+        gw = keep.tile([P, S], U32, name="gw", align_bytes=64)
+        for h in range(2):
+            nc.vector.tensor_copy(gw[:, h * HALF:(h + 1) * HALF], xw[:].indirect(offs_sb[:, h * 16:(h + 1) * 16]))
+
+        def project(t, lo, hi):
+            acc = psum.tile([P, BANK], F32, name="bank")
+            nc.tensor.matmul_mx(out=acc[:, 0:hi - lo], lhsT=w1_codes[t].bitcast(FP8X4), lhsT_scale=w1_scales[t],
+                                rhs=gw[:, lo:hi].bitcast(FP8X4), rhs_scale=gs[:, lo:hi], start=True, stop=True)
+            y = keep.tile([P, hi - lo], F32, name="y%d_%d" % (t, lo), align_bytes=64)
+            nc.scalar.copy(y[:], acc[:, 0:hi - lo])
+            return y
+
+        pieces = [(3, page3, 0, HALF), (3, page3, HALF, S), (1, page1, 0, S), (2, page23, 0, S), (0, page01, 0, S)]
+        ys = [project(t, lo, hi) for t, window, lo, hi in pieces]
+
+        def scatter(i):
+            t, window, lo, hi = pieces[i]
+            nc.vector.tensor_copy(window[:].indirect(slot_sb[:, lo // 16:hi // 16]), ys[i][:])
+
+        scatter(0)
+        scatter(1)
+
+        w2_grouped = keep.tile([P, N, PACK], BF16, name="w2_grouped", align_bytes=64)
+        nc.scalar.copy(w2_grouped[:].rearrange("p (c i) j -> p c j i", i=4), w2_raw[:].rearrange("p j (c i) -> p c j i", i=4))
+
+        nc.scalar.copy(page23[:, U:2 * U], page3[:])
+        scatter(2)
+        nc.scalar.copy(page01[:, U:2 * U], page1[:])
+        scatter(3)
+
+        w2_codes = keep.tile([P, N], U32, name="w2_codes", align_bytes=64)
+        w2_scales = keep.tile([P, N], U8, name="w2_scales", align_bytes=64)
+        nc.vector.quantize_mx(out=w2_codes[:].bitcast(FP8X4), scales=w2_scales[:], in_=w2_grouped[:].rearrange("p c j -> p (c j)"))
+
+        starts = [sum(CHUNKS[:i]) for i in range(len(CHUNKS))]
+        z_grouped = [keep.tile([P, cw, PACK], BF16, name="z_grouped%d" % i, align_bytes=64) for i, cw in enumerate(CHUNKS)]
+        src23 = page23[:].rearrange("p (h w) -> p w h", h=2)
+        src01 = page01[:].rearrange("p (h w) -> p w h", h=2)
+        for i, cw in enumerate(CHUNKS):
+            nc.scalar.copy(z_grouped[i][:, :, 2:4], src23[:, starts[i]:starts[i] + cw, :])
+        scatter(4)
+
+        z_codes = [keep.tile([P, cw], U32, name="z_codes%d" % i, align_bytes=64) for i, cw in enumerate(CHUNKS)]
+        z_scales = [keep.tile([P, cw], U8, name="z_scales%d" % i, align_bytes=64) for i, cw in enumerate(CHUNKS)]
+
+        def convert(i):
+            nc.vector.tensor_copy(z_grouped[i][:, :, 0:2], src01[:, starts[i]:starts[i] + CHUNKS[i], :])
+
+        def quantize(i):
+            nc.vector.quantize_mx(out=z_codes[i][:].bitcast(FP8X4), scales=z_scales[i][:], in_=z_grouped[i][:].rearrange("p w j -> p (w j)"))
+
+        out_rows = out.rearrange("(a p) w -> p a w", p=P)
+        units = []
+        for i, cw in enumerate(CHUNKS):
+            per_bank = 2 if i == 0 else BANK // cw
+            for a0 in range(0, N // P, per_bank):
+                units.append((i, a0, per_bank))
+
+        def multiply(u):
+            i, a0, count = units[u]
+            cw = CHUNKS[i]
+            acc = psum.tile([P, BANK], F32, name="bank")
+            for a in range(count):
+                m = slice((a0 + a) * P, (a0 + a + 1) * P)
+                nc.tensor.matmul_mx(out=acc[:, a * cw:(a + 1) * cw], lhsT=w2_codes[:, m].bitcast(FP8X4), lhsT_scale=w2_scales[:, m],
+                                    rhs=z_codes[i][:].bitcast(FP8X4), rhs_scale=z_scales[i][:], start=True, stop=True)
+            res = keep.tile([P, count * cw], F32, name="res%d" % u, align_bytes=64)
+            copy = nc.vector.tensor_copy if u >= len(units) - VECTOR_BANKS else nc.scalar.copy
+            copy(res[:], acc[:, 0:count * cw])
+            nc.sync.dma_start(out_rows[:, a0:a0 + count, starts[i]:starts[i] + cw], res[:].rearrange("p (a w) -> p a w", a=count))
+
+        convert(0)
+        for i in range(len(CHUNKS)):
+            if i + 1 < len(CHUNKS):
+                convert(i + 1)
+            quantize(i)
+        for u in range(len(units)):
+            multiply(u)

@@ -18,7 +18,8 @@ PACK = 4
 BANK = 512
 HALF = S // 2
 CHUNKS = (128, 128, 256, 256, 256)
-VECTOR_BANKS = 2
+STRIPS = ((0, 128, 2), (128, 128, 2), (256, 256, 2), (512, 512, 1))
+VECTOR_UNITS = (7, 9)
 
 
 def tile_picked_pagemix_none_p_kernel(tc, x_words, x_scales, w1, mem, w2, offs, slot, out):
@@ -32,26 +33,34 @@ def tile_picked_pagemix_none_p_kernel(tc, x_words, x_scales, w1, mem, w2, offs, 
         xw = keep.tile([P, T], U32, name="xw", align_bytes=64)
         xs = keep.tile([P, T], U8, name="xs", align_bytes=64)
         w1_raw = keep.tile([P, PACK, H], F32, name="w1_raw", align_bytes=64)
-        w2_raw = keep.tile([P, PACK, N], F32, name="w2_raw", align_bytes=64)
-        page3 = keep.tile([P, U], F32, name="page3", align_bytes=64)
-        page1 = keep.tile([P, U], F32, name="page1", align_bytes=64)
-        page23 = keep.tile([P, 2 * U], F32, name="page23", align_bytes=64)
-        page01 = keep.tile([P, 2 * U], F32, name="page01", align_bytes=64)
+        page3 = keep.tile([P, U], F32, name="page3", tag="page3", align_bytes=64)
 
         mem_rows = mem.rearrange("(p t) w -> t p w", t=PACK)
-        nc.vector.memset(xs[:].bitcast(I32), 0)
-        nc.sync.dma_start(offs_sb[:], offs)
-        nc.sync.dma_start(w1_raw[:], w1.rearrange("(p j) c -> p j c", j=PACK))
+        xs_landed = keep.tile([P, T], U8, name="xs_landed", align_bytes=64)
         scale_rows = x_scales[0].rearrange("(q r) c -> r q c", r=4)
+        nc.sync.dma_start(offs_sb[:], offs)
         for r in range(4):
-            nc.scalar.dma_start(xs[r:P:32, :].bitcast(I32), scale_rows[r].bitcast(I32))
+            queue = nc.scalar if r < 2 else nc.sync
+            queue.dma_start(xs_landed[r:P:32, :].bitcast(I32), scale_rows[r].bitcast(I32))
+        nc.sync.dma_start(w1_raw[:], w1.rearrange("(p j) c -> p j c", j=PACK))
         nc.sync.dma_start(xw[:].bitcast(I32), x_words[0].rearrange("p c r -> p (c r)").bitcast(I32))
         nc.sync.dma_start(slot_sb[:], slot)
         nc.sync.dma_start(page3[:], mem_rows[3])
+        page1 = keep.tile([P, U], F32, name="page1", tag="page1", align_bytes=64)
         nc.sync.dma_start(page1[:], mem_rows[1])
-        nc.sync.dma_start(w2_raw[:], w2.rearrange("(p j) c -> p j c", j=PACK))
+        page23 = keep.tile([P, 2 * U], F32, name="page23", align_bytes=64)
+        page01 = keep.tile([P, 2 * U], F32, name="page01", align_bytes=64)
+        w2_rows = w2.rearrange("(p j) c -> p j c", j=PACK)
+        w2_raw = [page[:, U:2 * U].rearrange("p (j c) -> p j c", j=PACK) for page in (page23, page01)]
+        for h in range(2):
+            nc.sync.dma_start(w2_raw[h], w2_rows[:, :, h * N // 2:(h + 1) * N // 2])
         nc.sync.dma_start(page23[:, 0:U], mem_rows[2])
         nc.sync.dma_start(page01[:, 0:U], mem_rows[0])
+
+        nc.vector.memset(xs[:].bitcast(I32), 0)
+        for q in range(4):
+            rows = slice(32 * q, 32 * q + 4)
+            nc.vector.tensor_copy(xs[rows, :].bitcast(I32), xs_landed[rows, :].bitcast(I32))
 
         gs = keep.tile([P, S], U8, name="gs", align_bytes=64)
         for h in range(2):
@@ -74,35 +83,45 @@ def tile_picked_pagemix_none_p_kernel(tc, x_words, x_scales, w1, mem, w2, offs, 
         for h in range(2):
             nc.vector.tensor_copy(gw[:, h * HALF:(h + 1) * HALF], xw[:].indirect(offs_sb[:, h * 16:(h + 1) * 16]))
 
-        def project(t, lo, hi):
-            acc = psum.tile([P, BANK], F32, name="bank")
-            nc.tensor.matmul_mx(out=acc[:, 0:hi - lo], lhsT=w1_codes[t].bitcast(FP8X4), lhsT_scale=w1_scales[t],
-                                rhs=gw[:, lo:hi].bitcast(FP8X4), rhs_scale=gs[:, lo:hi], start=True, stop=True)
-            y = keep.tile([P, hi - lo], F32, name="y%d_%d" % (t, lo), align_bytes=64)
-            nc.scalar.copy(y[:], acc[:, 0:hi - lo])
+        def project(t, cuts):
+            y = keep.tile([P, cuts[-1] - cuts[0]], F32, name="y%d_%d" % (t, cuts[0]), align_bytes=64)
+            for lo, hi in zip(cuts, cuts[1:]):
+                acc = psum.tile([P, BANK], F32, name="bank")
+                nc.tensor.matmul_mx(out=acc[:, 0:hi - lo], lhsT=w1_codes[t].bitcast(FP8X4), lhsT_scale=w1_scales[t],
+                                    rhs=gw[:, lo:hi].bitcast(FP8X4), rhs_scale=gs[:, lo:hi], start=True, stop=True)
+                nc.scalar.copy(y[:, lo - cuts[0]:hi - cuts[0]], acc[:, 0:hi - lo])
             return y
 
-        pieces = [(3, page3, 0, HALF), (3, page3, HALF, S), (1, page1, 0, S), (2, page23, 0, S), (0, page01, 0, S)]
-        ys = [project(t, lo, hi) for t, window, lo, hi in pieces]
+        pieces = [(3, (0, 128)), (3, (128, HALF, S)), (1, (0, S)), (2, (0, S)), (0, (0, S))]
+        ys = [project(t, cuts) for t, cuts in pieces]
 
-        def scatter(i):
-            t, window, lo, hi = pieces[i]
-            nc.vector.tensor_copy(window[:].indirect(slot_sb[:, lo // 16:hi // 16]), ys[i][:])
+        def scatter(i, window):
+            t, cuts = pieces[i]
+            nc.vector.tensor_copy(window[:].indirect(slot_sb[:, cuts[0] // 16:cuts[-1] // 16]), ys[i][:])
 
-        scatter(0)
-        scatter(1)
+        scatter(0, page3)
+        scatter(1, page3)
 
-        w2_grouped = keep.tile([P, N, PACK], BF16, name="w2_grouped", align_bytes=64)
-        nc.scalar.copy(w2_grouped[:].rearrange("p (c i) j -> p c j i", i=4), w2_raw[:].rearrange("p j (c i) -> p c j i", i=4))
+        w2_grouped = []
 
+        def round_w2(h):
+            w2_grouped.append(keep.tile([P, N // 2, PACK], BF16, name="w2_grouped%d" % h, tag=("w2_grouped0", "page3")[h], align_bytes=64))
+            nc.scalar.copy(w2_grouped[h][:].rearrange("p (c i) j -> p c j i", i=4), w2_raw[h].rearrange("p j (c i) -> p c j i", i=4))
+
+        round_w2(0)
         nc.scalar.copy(page23[:, U:2 * U], page3[:])
-        scatter(2)
-        nc.scalar.copy(page01[:, U:2 * U], page1[:])
-        scatter(3)
+        round_w2(1)
 
-        w2_codes = keep.tile([P, N], U32, name="w2_codes", align_bytes=64)
+        scatter(2, page1)
+        nc.scalar.copy(page01[:, U:2 * U], page1[:])
+        scatter(3, page23)
+
+        w2_codes = keep.tile([P, N], U32, name="w2_codes", tag="page1", align_bytes=64)
         w2_scales = keep.tile([P, N], U8, name="w2_scales", align_bytes=64)
-        nc.vector.quantize_mx(out=w2_codes[:].bitcast(FP8X4), scales=w2_scales[:], in_=w2_grouped[:].rearrange("p c j -> p (c j)"))
+
+        def quantize_w2(h):
+            cols = slice(h * N // 2, (h + 1) * N // 2)
+            nc.vector.quantize_mx(out=w2_codes[:, cols].bitcast(FP8X4), scales=w2_scales[:, cols], in_=w2_grouped[h][:].rearrange("p c j -> p (c j)"))
 
         starts = [sum(CHUNKS[:i]) for i in range(len(CHUNKS))]
         z_grouped = [keep.tile([P, cw, PACK], BF16, name="z_grouped%d" % i, align_bytes=64) for i, cw in enumerate(CHUNKS)]
@@ -110,41 +129,46 @@ def tile_picked_pagemix_none_p_kernel(tc, x_words, x_scales, w1, mem, w2, offs, 
         src01 = page01[:].rearrange("p (h w) -> p w h", h=2)
         for i, cw in enumerate(CHUNKS):
             nc.scalar.copy(z_grouped[i][:, :, 2:4], src23[:, starts[i]:starts[i] + cw, :])
-        scatter(4)
+        scatter(4, page01)
 
-        z_codes = [keep.tile([P, cw], U32, name="z_codes%d" % i, align_bytes=64) for i, cw in enumerate(CHUNKS)]
-        z_scales = [keep.tile([P, cw], U8, name="z_scales%d" % i, align_bytes=64) for i, cw in enumerate(CHUNKS)]
+        z_codes = keep.tile([P, U], U32, name="z_codes", align_bytes=64)
+        z_scales = keep.tile([P, U], U8, name="z_scales", align_bytes=64)
 
         def convert(i):
             nc.vector.tensor_copy(z_grouped[i][:, :, 0:2], src01[:, starts[i]:starts[i] + CHUNKS[i], :])
 
         def quantize(i):
-            nc.vector.quantize_mx(out=z_codes[i][:].bitcast(FP8X4), scales=z_scales[i][:], in_=z_grouped[i][:].rearrange("p w j -> p (w j)"))
+            nc.vector.quantize_mx(out=z_codes[:, starts[i]:starts[i] + CHUNKS[i]].bitcast(FP8X4), scales=z_scales[:, starts[i]:starts[i] + CHUNKS[i]], in_=z_grouped[i][:].rearrange("p w j -> p (w j)"))
 
         out_rows = out.rearrange("(a p) w -> p a w", p=P)
         units = []
-        for i, cw in enumerate(CHUNKS):
-            per_bank = 2 if i == 0 else BANK // cw
-            for a0 in range(0, N // P, per_bank):
-                units.append((i, a0, per_bank))
+        for w0, cw, count in STRIPS:
+            for a0 in range(0, N // P, count):
+                units.append((w0, cw, a0, count))
 
         def multiply(u):
-            i, a0, count = units[u]
-            cw = CHUNKS[i]
+            w0, cw, a0, count = units[u]
             acc = psum.tile([P, BANK], F32, name="bank")
             for a in range(count):
                 m = slice((a0 + a) * P, (a0 + a + 1) * P)
                 nc.tensor.matmul_mx(out=acc[:, a * cw:(a + 1) * cw], lhsT=w2_codes[:, m].bitcast(FP8X4), lhsT_scale=w2_scales[:, m],
-                                    rhs=z_codes[i][:].bitcast(FP8X4), rhs_scale=z_scales[i][:], start=True, stop=True)
+                                    rhs=z_codes[:, w0:w0 + cw].bitcast(FP8X4), rhs_scale=z_scales[:, w0:w0 + cw], start=True, stop=True)
             res = keep.tile([P, count * cw], F32, name="res%d" % u, align_bytes=64)
-            copy = nc.vector.tensor_copy if u >= len(units) - VECTOR_BANKS else nc.scalar.copy
+            copy = nc.vector.tensor_copy if u in VECTOR_UNITS else nc.scalar.copy
             copy(res[:], acc[:, 0:count * cw])
-            nc.sync.dma_start(out_rows[:, a0:a0 + count, starts[i]:starts[i] + cw], res[:].rearrange("p (a w) -> p a w", a=count))
+            nc.sync.dma_start(out_rows[:, a0:a0 + count, w0:w0 + cw], res[:].rearrange("p (a w) -> p a w", a=count))
 
+        quantize_w2(0)
         convert(0)
-        for i in range(len(CHUNKS)):
-            if i + 1 < len(CHUNKS):
-                convert(i + 1)
-            quantize(i)
+        quantize_w2(1)
+        quantize(0)
+        convert(1)
+        convert(2)
+        quantize(1)
+        quantize(2)
+        convert(3)
+        convert(4)
+        quantize(3)
+        quantize(4)
         for u in range(len(units)):
             multiply(u)

@@ -54,8 +54,8 @@ def tile_picked_pagemix_none_p_kernel(tc, x_words, x_scales, w1, mem, w2, offs, 
         w2_raw = [page[:, U:2 * U].rearrange("p (j c) -> p j c", j=PACK) for page in (page23, page01)]
         for h in range(2):
             nc.sync.dma_start(w2_raw[h], w2_rows[:, :, h * N // 2:(h + 1) * N // 2])
-        nc.sync.dma_start(page23[:, 0:U], mem_rows[2])
         nc.sync.dma_start(page01[:, 0:U], mem_rows[0])
+        nc.sync.dma_start(page23[:, 0:U], mem_rows[2])
 
         nc.vector.memset(xs[:].bitcast(I32), 0)
         for q in range(4):

@@ -18,8 +18,8 @@ PACK = 4
 BANK = 512
 HALF = S // 2
 CHUNKS = (128, 128, 256, 256, 256)
-STRIPS = ((0, 128, 2), (128, 128, 2), (256, 256, 2), (512, 512, 1))
-VECTOR_UNITS = (7, 9)
+STRIPS = ((0, 128, 2), (128, 128, 2), (256, 256, 1), (512, 512, 1))
+VECTOR_UNITS = (9, 11)
 
 
 def tile_picked_pagemix_none_p_kernel(tc, x_words, x_scales, w1, mem, w2, offs, slot, out):
@@ -135,7 +135,8 @@ def tile_picked_pagemix_none_p_kernel(tc, x_words, x_scales, w1, mem, w2, offs, 
         z_scales = keep.tile([P, U], U8, name="z_scales", align_bytes=64)
 
         def convert(i):
-            nc.vector.tensor_copy(z_grouped[i][:, :, 0:2], src01[:, starts[i]:starts[i] + CHUNKS[i], :])
+            copy = nc.scalar.copy if i == len(CHUNKS) - 1 else nc.vector.tensor_copy
+            copy(z_grouped[i][:, :, 0:2], src01[:, starts[i]:starts[i] + CHUNKS[i], :])
 
         def quantize(i):
             nc.vector.quantize_mx(out=z_codes[:, starts[i]:starts[i] + CHUNKS[i]].bitcast(FP8X4), scales=z_scales[:, starts[i]:starts[i] + CHUNKS[i]], in_=z_grouped[i][:].rearrange("p w j -> p (w j)"))

@@ -18,8 +18,6 @@ PACK = 4
 BANK = 512
 HALF = S // 2
 CHUNKS = (128, 128, 256, 256, 256)
-STRIPS = ((0, 128, 2), (128, 128, 2), (256, 256, 1), (512, 512, 1))
-VECTOR_UNITS = (9, 11)
 
 
 def tile_picked_pagemix_none_p_kernel(tc, x_words, x_scales, w1, mem, w2, offs, slot, out):
@@ -84,7 +82,7 @@ def tile_picked_pagemix_none_p_kernel(tc, x_words, x_scales, w1, mem, w2, offs, 
             nc.vector.tensor_copy(gw[:, h * HALF:(h + 1) * HALF], xw[:].indirect(offs_sb[:, h * 16:(h + 1) * 16]))
 
         def project(t, cuts):
-            y = keep.tile([P, cuts[-1] - cuts[0]], F32, name="y%d_%d" % (t, cuts[0]), align_bytes=64)
+            y = keep.tile([P, cuts[-1] - cuts[0]], F32, name="y%d_%d" % (t, cuts[0]), tag="y%d_%d" % (t, cuts[0]), align_bytes=64)
             for lo, hi in zip(cuts, cuts[1:]):
                 acc = psum.tile([P, BANK], F32, name="bank")
                 nc.tensor.matmul_mx(out=acc[:, 0:hi - lo], lhsT=w1_codes[t].bitcast(FP8X4), lhsT_scale=w1_scales[t],
@@ -116,15 +114,16 @@ def tile_picked_pagemix_none_p_kernel(tc, x_words, x_scales, w1, mem, w2, offs, 
         nc.scalar.copy(page01[:, U:2 * U], page1[:])
         scatter(3, page23)
 
-        w2_codes = keep.tile([P, N], U32, name="w2_codes", tag="page1", align_bytes=64)
-        w2_scales = keep.tile([P, N], U8, name="w2_scales", align_bytes=64)
+        w2_codes = []
+        w2_scales = []
 
         def quantize_w2(h):
-            cols = slice(h * N // 2, (h + 1) * N // 2)
-            nc.vector.quantize_mx(out=w2_codes[:, cols].bitcast(FP8X4), scales=w2_scales[:, cols], in_=w2_grouped[h][:].rearrange("p c j -> p (c j)"))
+            w2_codes.append(keep.tile([P, N // 2], U32, name="w2_codes%d" % h, tag=("page1", "y0_0")[h], align_bytes=64))
+            w2_scales.append(keep.tile([P, N // 2], U8, name="w2_scales%d" % h, align_bytes=64))
+            nc.vector.quantize_mx(out=w2_codes[h][:].bitcast(FP8X4), scales=w2_scales[h][:], in_=w2_grouped[h][:].rearrange("p c j -> p (c j)"))
 
         starts = [sum(CHUNKS[:i]) for i in range(len(CHUNKS))]
-        z_grouped = [keep.tile([P, cw, PACK], BF16, name="z_grouped%d" % i, align_bytes=64) for i, cw in enumerate(CHUNKS)]
+        z_grouped = [keep.tile([P, cw, PACK], BF16, name="z_grouped%d" % i, tag="z_grouped%d" % i, align_bytes=64) for i, cw in enumerate(CHUNKS)]
         src23 = page23[:].rearrange("p (h w) -> p w h", h=2)
         src01 = page01[:].rearrange("p (h w) -> p w h", h=2)
         for i, cw in enumerate(CHUNKS):
@@ -142,22 +141,20 @@ def tile_picked_pagemix_none_p_kernel(tc, x_words, x_scales, w1, mem, w2, offs, 
             nc.vector.quantize_mx(out=z_codes[:, starts[i]:starts[i] + CHUNKS[i]].bitcast(FP8X4), scales=z_scales[:, starts[i]:starts[i] + CHUNKS[i]], in_=z_grouped[i][:].rearrange("p w j -> p (w j)"))
 
         out_rows = out.rearrange("(a p) w -> p a w", p=P)
-        units = []
-        for w0, cw, count in STRIPS:
-            for a0 in range(0, N // P, count):
-                units.append((w0, cw, a0, count))
 
-        def multiply(u):
-            w0, cw, a0, count = units[u]
+        def multiply(copy, res, tiles, w0, cw):
             acc = psum.tile([P, BANK], F32, name="bank")
-            for a in range(count):
-                m = slice((a0 + a) * P, (a0 + a + 1) * P)
-                nc.tensor.matmul_mx(out=acc[:, a * cw:(a + 1) * cw], lhsT=w2_codes[:, m].bitcast(FP8X4), lhsT_scale=w2_scales[:, m],
+            for i, a in enumerate(tiles):
+                m = slice(a % 2 * P, (a % 2 + 1) * P)
+                nc.tensor.matmul_mx(out=acc[:, i * cw:(i + 1) * cw], lhsT=w2_codes[a // 2][:, m].bitcast(FP8X4), lhsT_scale=w2_scales[a // 2][:, m],
                                     rhs=z_codes[:, w0:w0 + cw].bitcast(FP8X4), rhs_scale=z_scales[:, w0:w0 + cw], start=True, stop=True)
-            res = keep.tile([P, count * cw], F32, name="res%d" % u, align_bytes=64)
-            copy = nc.vector.tensor_copy if u in VECTOR_UNITS else nc.scalar.copy
-            copy(res[:], acc[:, 0:count * cw])
-            nc.sync.dma_start(out_rows[:, a0:a0 + count, w0:w0 + cw], res[:].rearrange("p (a w) -> p a w", a=count))
+            copy(res, acc[:, 0:len(tiles) * cw])
+
+        def strip(copy, tiles, i, tag):
+            w0, cw = starts[i], CHUNKS[i]
+            res = keep.tile([P, len(tiles) * cw], F32, name=tag, tag=tag, align_bytes=64)
+            multiply(copy, res[:], tiles, w0, cw)
+            nc.sync.dma_start(out_rows[:, tiles[0]:tiles[-1] + 1, w0:w0 + cw], res[:].rearrange("p (a w) -> p a w", a=len(tiles)))
 
         quantize_w2(0)
         convert(0)
@@ -169,7 +166,20 @@ def tile_picked_pagemix_none_p_kernel(tc, x_words, x_scales, w1, mem, w2, offs, 
         quantize(2)
         convert(3)
         convert(4)
-        quantize(3)
         quantize(4)
-        for u in range(len(units)):
-            multiply(u)
+        quantize(3)
+        for a in range(4):
+            strip(nc.scalar.copy, (a,), 0, "res0_%d" % a)
+        strip(nc.scalar.copy, (0, 1), 1, "res1_0")
+        strip(nc.scalar.copy, (2, 3), 1, "res1_2")
+        strip(nc.scalar.copy, (0,), 2, "res2_0")
+        strip(nc.scalar.copy, (1,), 2, "res2_1")
+        res = keep.tile([P, 2 * HALF], F32, name="res2_2", tag="z_grouped3", align_bytes=64)
+        for i in range(2):
+            multiply(nc.vector.tensor_copy, res[:, i * HALF:(i + 1) * HALF], (2 + i,), starts[2], HALF)
+        nc.sync.dma_start(out_rows[:, 2:4, starts[2]:starts[3]], res[:].rearrange("p (a w) -> p a w", a=2))
+        for a in range(4):
+            res = keep.tile([P, BANK], F32, name="rows%d" % a, align_bytes=64)
+            multiply(nc.scalar.copy, res[:, HALF:BANK], (a,), starts[4], HALF)
+            multiply(nc.vector.tensor_copy, res[:, 0:HALF], (a,), starts[3], HALF)
+            nc.sync.dma_start(out_rows[:, a, BANK:U], res[:])

@@ -24,45 +24,35 @@ def tile_picked_pagemix_none_p_kernel(tc, x_words, x_scales, w1, mem, w2, offs, 
     nc = tc.nc
     with ExitStack() as ctx:
         keep = ctx.enter_context(tc.tile_pool(name="keep", bufs=1))
+        shared = ctx.enter_context(tc.tile_pool(name="shared", bufs=1))
         psum = ctx.enter_context(tc.psum_pool(name="psum", bufs=8))
 
         offs_sb = keep.tile([P, S // 16], U16, name="offs_sb")
         slot_sb = keep.tile([P, S // 16], U16, name="slot_sb")
         xw = keep.tile([P, T], U32, name="xw", align_bytes=64)
-        xs = keep.tile([P, T], U8, name="xs", align_bytes=64)
-        w1_raw = keep.tile([P, PACK, H], F32, name="w1_raw", align_bytes=64)
-        page3 = keep.tile([P, U], F32, name="page3", tag="page3", align_bytes=64)
+        xs = shared.tile([P, T], U8, name="xs", align_bytes=64, offset=3072)
+        w1_raw = shared.tile([P, PACK, H], F32, name="w1_raw", align_bytes=64, offset=12288)
 
         mem_rows = mem.rearrange("(p t) w -> t p w", t=PACK)
-        xs_landed = keep.tile([P, T], U8, name="xs_landed", align_bytes=64)
-        scale_rows = x_scales[0].rearrange("(q r) c -> r q c", r=4)
+        nc.sync.dma_start(xs[16:32, :].bitcast(I32), x_scales[0].bitcast(I32))
         nc.sync.dma_start(offs_sb[:], offs)
-        for r in range(4):
-            queue = nc.scalar if r < 2 else nc.sync
-            queue.dma_start(xs_landed[r:P:32, :].bitcast(I32), scale_rows[r].bitcast(I32))
         nc.sync.dma_start(w1_raw[:], w1.rearrange("(p j) c -> p j c", j=PACK))
         nc.sync.dma_start(xw[:].bitcast(I32), x_words[0].rearrange("p c r -> p (c r)").bitcast(I32))
         nc.sync.dma_start(slot_sb[:], slot)
-        nc.sync.dma_start(page3[:], mem_rows[3])
-        page1 = keep.tile([P, U], F32, name="page1", tag="page1", align_bytes=64)
-        nc.sync.dma_start(page1[:], mem_rows[1])
-        page23 = keep.tile([P, 2 * U], F32, name="page23", align_bytes=64)
-        page01 = keep.tile([P, 2 * U], F32, name="page01", align_bytes=64)
-        w2_rows = w2.rearrange("(p j) c -> p j c", j=PACK)
-        w2_raw = [page[:, U:2 * U].rearrange("p (j c) -> p j c", j=PACK) for page in (page23, page01)]
-        for h in range(2):
-            nc.sync.dma_start(w2_raw[h], w2_rows[:, :, h * N // 2:(h + 1) * N // 2])
-        nc.sync.dma_start(page01[:, 0:U], mem_rows[0])
-        nc.sync.dma_start(page23[:, 0:U], mem_rows[2])
 
-        nc.vector.memset(xs[:].bitcast(I32), 0)
-        for q in range(4):
-            rows = slice(32 * q, 32 * q + 4)
-            nc.vector.tensor_copy(xs[rows, :].bitcast(I32), xs_landed[rows, :].bitcast(I32))
-
+        for rows in (slice(0, 16), slice(32, 64), slice(64, P)):
+            nc.vector.memset(xs[rows, :].bitcast(I32), 0)
         gs = keep.tile([P, S], U8, name="gs", align_bytes=64)
-        for h in range(2):
-            nc.vector.tensor_copy(gs[:, h * HALF:(h + 1) * HALF], xs[:].indirect(offs_sb[:, h * 16:(h + 1) * 16]))
+        nc.vector.memset(gs[:].bitcast(I32), 0)
+        picked = keep.tile([P, S], U8, name="picked", align_bytes=64)
+        nc.vector.tensor_copy(picked[:], xs[:].indirect(offs_sb[:]))
+        for q in range(4):
+            nc.sync.dma_start(gs[32 * q:32 * q + 4, :].bitcast(I32), picked[16 + 4 * q:20 + 4 * q, :].bitcast(I32))
+
+        page3 = shared.tile([P, U], F32, name="page3", tag="page3", align_bytes=64, offset=0)
+        nc.sync.dma_start(page3[:], mem_rows[3])
+        page1 = shared.tile([P, U], F32, name="page1", tag="page1", align_bytes=64, offset=4096)
+        nc.sync.dma_start(page1[:], mem_rows[1])
 
         w1_src = w1_raw[:].rearrange("p j (m t) -> p m j t", t=PACK)
         w1_codes = {}
@@ -76,6 +66,15 @@ def tile_picked_pagemix_none_p_kernel(tc, x_words, x_scales, w1, mem, w2, offs, 
             for i in range(2):
                 w1_codes[t0 + i] = codes[:, i * P:(i + 1) * P]
                 w1_scales[t0 + i] = scales[:, i * P:(i + 1) * P]
+
+        page23 = shared.tile([P, 2 * U], F32, name="page23", align_bytes=64, offset=8192)
+        page01 = shared.tile([P, 2 * U], F32, name="page01", align_bytes=64, offset=16384)
+        w2_rows = w2.rearrange("(p j) c -> p j c", j=PACK)
+        w2_raw = [page[:, U:2 * U].rearrange("p (j c) -> p j c", j=PACK) for page in (page23, page01)]
+        for h in range(2):
+            nc.sync.dma_start(w2_raw[h], w2_rows[:, :, h * N // 2:(h + 1) * N // 2])
+        nc.sync.dma_start(page01[:, 0:U], mem_rows[0])
+        nc.sync.dma_start(page23[:, 0:U], mem_rows[2])
 
         gw = keep.tile([P, S], U32, name="gw", align_bytes=64)
         for h in range(2):
@@ -103,7 +102,7 @@ def tile_picked_pagemix_none_p_kernel(tc, x_words, x_scales, w1, mem, w2, offs, 
         w2_grouped = []
 
         def round_w2(h):
-            w2_grouped.append(keep.tile([P, N // 2, PACK], BF16, name="w2_grouped%d" % h, tag=("w2_grouped0", "page3")[h], align_bytes=64))
+            w2_grouped.append(shared.tile([P, N // 2, PACK], BF16, name="w2_grouped%d" % h, tag=("w2_grouped0", "page3")[h], align_bytes=64, offset=(24576, 0)[h]))
             nc.scalar.copy(w2_grouped[h][:].rearrange("p (c i) j -> p c j i", i=4), w2_raw[h].rearrange("p j (c i) -> p c j i", i=4))
 
         round_w2(0)
@@ -118,7 +117,10 @@ def tile_picked_pagemix_none_p_kernel(tc, x_words, x_scales, w1, mem, w2, offs, 
         w2_scales = []
 
         def quantize_w2(h):
-            w2_codes.append(keep.tile([P, N // 2], U32, name="w2_codes%d" % h, tag=("page1", "y0_0")[h], align_bytes=64))
+            if h == 0:
+                w2_codes.append(shared.tile([P, N // 2], U32, name="w2_codes0", tag="page1", align_bytes=64, offset=4096))
+            else:
+                w2_codes.append(keep.tile([P, N // 2], U32, name="w2_codes1", tag="y0_0", align_bytes=64))
             w2_scales.append(keep.tile([P, N // 2], U8, name="w2_scales%d" % h, align_bytes=64))
             nc.vector.quantize_mx(out=w2_codes[h][:].bitcast(FP8X4), scales=w2_scales[h][:], in_=w2_grouped[h][:].rearrange("p c j -> p (c j)"))
 

@@ -34,11 +34,11 @@ def tile_picked_pagemix_none_p_kernel(tc, x_words, x_scales, w1, mem, w2, offs, 
         w1_raw = shared.tile([P, PACK, H], F32, name="w1_raw", align_bytes=64, offset=12288)
 
         mem_rows = mem.rearrange("(p t) w -> t p w", t=PACK)
-        nc.sync.dma_start(xs[16:32, :].bitcast(I32), x_scales[0].bitcast(I32))
+        nc.scalar.dma_start(xs[16:32, :].bitcast(I32), x_scales[0].bitcast(I32))
         nc.sync.dma_start(offs_sb[:], offs)
+        nc.sync.dma_start(slot_sb[:], slot)
         nc.sync.dma_start(w1_raw[:], w1.rearrange("(p j) c -> p j c", j=PACK))
         nc.sync.dma_start(xw[:].bitcast(I32), x_words[0].rearrange("p c r -> p (c r)").bitcast(I32))
-        nc.sync.dma_start(slot_sb[:], slot)
 
         for rows in (slice(0, 16), slice(32, 64), slice(64, P)):
             nc.vector.memset(xs[rows, :].bitcast(I32), 0)
@@ -165,23 +165,21 @@ def tile_picked_pagemix_none_p_kernel(tc, x_words, x_scales, w1, mem, w2, offs, 
         convert(1)
         convert(2)
         quantize(1)
-        quantize(2)
         convert(3)
-        convert(4)
-        quantize(4)
+        quantize(2)
         quantize(3)
-        for a in range(4):
-            strip(nc.scalar.copy, (a,), 0, "res0_%d" % a)
+        convert(4)
+        strip(nc.scalar.copy, (0,), 0, "res0_0")
+        strip(nc.scalar.copy, (1,), 0, "res0_1")
+        strip(nc.scalar.copy, (2, 3), 0, "res0_2")
         strip(nc.scalar.copy, (0, 1), 1, "res1_0")
-        strip(nc.scalar.copy, (2, 3), 1, "res1_2")
-        strip(nc.scalar.copy, (0,), 2, "res2_0")
-        strip(nc.scalar.copy, (1,), 2, "res2_1")
-        res = keep.tile([P, 2 * HALF], F32, name="res2_2", tag="z_grouped3", align_bytes=64)
-        for i in range(2):
-            multiply(nc.vector.tensor_copy, res[:, i * HALF:(i + 1) * HALF], (2 + i,), starts[2], HALF)
-        nc.sync.dma_start(out_rows[:, 2:4, starts[2]:starts[3]], res[:].rearrange("p (a w) -> p a w", a=2))
+        strip(nc.vector.tensor_copy, (2, 3), 1, "res1_2")
+        quantize(4)
         for a in range(4):
-            res = keep.tile([P, BANK], F32, name="rows%d" % a, align_bytes=64)
-            multiply(nc.scalar.copy, res[:, HALF:BANK], (a,), starts[4], HALF)
-            multiply(nc.vector.tensor_copy, res[:, 0:HALF], (a,), starts[3], HALF)
-            nc.sync.dma_start(out_rows[:, a, BANK:U], res[:])
+            strip(nc.vector.tensor_copy if a == 2 else nc.scalar.copy, (a,), 2, "res2_%d" % a)
+        for tiles in ((0,), (1,), (2, 3)):
+            res = keep.tile([P, len(tiles), BANK], F32, name="rows%d" % tiles[0], align_bytes=64)
+            for i, a in enumerate(tiles):
+                multiply(nc.vector.tensor_copy, res[:, i, 0:HALF], (a,), starts[3], HALF)
+                multiply(nc.scalar.copy, res[:, i, HALF:BANK], (a,), starts[4], HALF)
+            nc.sync.dma_start(out_rows[:, tiles[0]:tiles[-1] + 1, BANK:U], res[:])

@@ -160,24 +160,27 @@ def tile_picked_pagemix_none_p_kernel(tc, x_words, x_scales, w1, mem, w2, offs, 
 
         quantize_w2(0)
         convert(0)
-        quantize_w2(1)
-        quantize(0)
         convert(1)
-        convert(2)
+        quantize(0)
         quantize(1)
+        quantize_w2(1)
+        convert(2)
         convert(3)
         quantize(2)
         quantize(3)
         convert(4)
-        strip(nc.scalar.copy, (0,), 0, "res0_0")
-        strip(nc.scalar.copy, (1,), 0, "res0_1")
-        strip(nc.scalar.copy, (2, 3), 0, "res0_2")
-        strip(nc.scalar.copy, (0, 1), 1, "res1_0")
-        strip(nc.vector.tensor_copy, (2, 3), 1, "res1_2")
-        quantize(4)
         for a in range(4):
-            strip(nc.vector.tensor_copy if a == 2 else nc.scalar.copy, (a,), 2, "res2_%d" % a)
-        for tiles in ((0,), (1,), (2, 3)):
+            res = keep.tile([P, HALF], F32, name="res0_%d" % a, align_bytes=64)
+            multiply(nc.vector.tensor_copy if a == 3 else nc.scalar.copy, res[:], (a,), 0, HALF)
+            nc.sync.dma_start(out_rows[:, a, 0:HALF], res[:])
+        quantize(4)
+        strip(nc.scalar.copy, (0,), 2, "res2_0")
+        strip(nc.scalar.copy, (1,), 2, "res2_1")
+        res = keep.tile([P, 2, HALF], F32, name="res2_2", align_bytes=64)
+        multiply(nc.vector.tensor_copy, res[:, 0, :], (2,), starts[2], HALF)
+        multiply(nc.scalar.copy, res[:, 1, :], (3,), starts[2], HALF)
+        nc.sync.dma_start(out_rows[:, 2:4, starts[2]:starts[3]], res[:])
+        for tiles in ((0, 1), (2, 3)):
             res = keep.tile([P, len(tiles), BANK], F32, name="rows%d" % tiles[0], align_bytes=64)
             for i, a in enumerate(tiles):
                 multiply(nc.vector.tensor_copy, res[:, i, 0:HALF], (a,), starts[3], HALF)

@@ -17,7 +17,7 @@ P = 128
 PACK = 4
 BANK = 512
 HALF = S // 2
-CHUNKS = (128, 128, 256, 256, 256)
+CHUNKS = (128, 128, 128, 128, 256, 256)
 
 
 def tile_picked_pagemix_none_p_kernel(tc, x_words, x_scales, w1, mem, w2, offs, slot, out):
@@ -25,7 +25,7 @@ def tile_picked_pagemix_none_p_kernel(tc, x_words, x_scales, w1, mem, w2, offs, 
     with ExitStack() as ctx:
         keep = ctx.enter_context(tc.tile_pool(name="keep", bufs=1))
         shared = ctx.enter_context(tc.tile_pool(name="shared", bufs=1))
-        psum = ctx.enter_context(tc.psum_pool(name="psum", bufs=8))
+        psum = ctx.enter_context(tc.psum_pool(name="psum", bufs=1))
 
         offs_sb = keep.tile([P, S // 16], U16, name="offs_sb")
         slot_sb = keep.tile([P, S // 16], U16, name="slot_sb")
@@ -80,10 +80,16 @@ def tile_picked_pagemix_none_p_kernel(tc, x_words, x_scales, w1, mem, w2, offs, 
         for h in range(2):
             nc.vector.tensor_copy(gw[:, h * HALF:(h + 1) * HALF], xw[:].indirect(offs_sb[:, h * 16:(h + 1) * 16]))
 
+        def bank(b):
+            return psum.tile([P, BANK], F32, name="bank%d" % b, tag="bank%d" % b)
+
+        used = []
+
         def project(t, cuts):
             y = keep.tile([P, cuts[-1] - cuts[0]], F32, name="y%d_%d" % (t, cuts[0]), tag="y%d_%d" % (t, cuts[0]), align_bytes=64)
             for lo, hi in zip(cuts, cuts[1:]):
-                acc = psum.tile([P, BANK], F32, name="bank")
+                acc = bank(len(used))
+                used.append(lo)
                 nc.tensor.matmul_mx(out=acc[:, 0:hi - lo], lhsT=w1_codes[t].bitcast(FP8X4), lhsT_scale=w1_scales[t],
                                     rhs=gw[:, lo:hi].bitcast(FP8X4), rhs_scale=gs[:, lo:hi], start=True, stop=True)
                 nc.scalar.copy(y[:, lo - cuts[0]:hi - cuts[0]], acc[:, 0:hi - lo])
@@ -113,30 +119,35 @@ def tile_picked_pagemix_none_p_kernel(tc, x_words, x_scales, w1, mem, w2, offs, 
         nc.scalar.copy(page01[:, U:2 * U], page1[:])
         scatter(3, page23)
 
-        w2_codes = []
-        w2_scales = []
+        w2_codes = {}
+        w2_scales = {}
 
-        def quantize_w2(h):
-            if h == 0:
-                w2_codes.append(shared.tile([P, N // 2], U32, name="w2_codes0", tag="page1", align_bytes=64, offset=4096))
+        def quantize_w2(tiles):
+            width = len(tiles) * P
+            if tiles[0] == 0:
+                codes = shared.tile([P, width], U32, name="w2_codes0", tag="page1", align_bytes=64, offset=4096)
             else:
-                w2_codes.append(keep.tile([P, N // 2], U32, name="w2_codes1", tag="y0_0", align_bytes=64))
-            w2_scales.append(keep.tile([P, N // 2], U8, name="w2_scales%d" % h, align_bytes=64))
-            nc.vector.quantize_mx(out=w2_codes[h][:].bitcast(FP8X4), scales=w2_scales[h][:], in_=w2_grouped[h][:].rearrange("p c j -> p (c j)"))
+                codes = keep.tile([P, width], U32, name="w2_codes%d" % tiles[0], tag=("y0_0", "z_grouped5")[tiles[0] - 1], align_bytes=64)
+            scales = keep.tile([P, width], U8, name="w2_scales%d" % tiles[0], align_bytes=64)
+            c0 = tiles[0] % 2 * P
+            nc.vector.quantize_mx(out=codes[:].bitcast(FP8X4), scales=scales[:], in_=w2_grouped[tiles[0] // 2][:, c0:c0 + width, :].rearrange("p c j -> p (c j)"))
+            for i, a in enumerate(tiles):
+                w2_codes[a] = codes[:, i * P:(i + 1) * P]
+                w2_scales[a] = scales[:, i * P:(i + 1) * P]
 
         starts = [sum(CHUNKS[:i]) for i in range(len(CHUNKS))]
         z_grouped = [keep.tile([P, cw, PACK], BF16, name="z_grouped%d" % i, tag="z_grouped%d" % i, align_bytes=64) for i, cw in enumerate(CHUNKS)]
         src23 = page23[:].rearrange("p (h w) -> p w h", h=2)
         src01 = page01[:].rearrange("p (h w) -> p w h", h=2)
-        for i, cw in enumerate(CHUNKS):
-            nc.scalar.copy(z_grouped[i][:, :, 2:4], src23[:, starts[i]:starts[i] + cw, :])
+        for i in range(len(CHUNKS)):
+            nc.scalar.copy(z_grouped[i][:, :, 2:4], src23[:, starts[i]:starts[i] + CHUNKS[i], :])
         scatter(4, page01)
 
         z_codes = keep.tile([P, U], U32, name="z_codes", align_bytes=64)
         z_scales = keep.tile([P, U], U8, name="z_scales", align_bytes=64)
 
         def convert(i):
-            copy = nc.scalar.copy if i == len(CHUNKS) - 1 else nc.vector.tensor_copy
+            copy = nc.scalar.copy if i >= 4 else nc.vector.tensor_copy
             copy(z_grouped[i][:, :, 0:2], src01[:, starts[i]:starts[i] + CHUNKS[i], :])
 
         def quantize(i):
@@ -144,45 +155,43 @@ def tile_picked_pagemix_none_p_kernel(tc, x_words, x_scales, w1, mem, w2, offs, 
 
         out_rows = out.rearrange("(a p) w -> p a w", p=P)
 
-        def multiply(copy, res, tiles, w0, cw):
-            acc = psum.tile([P, BANK], F32, name="bank")
-            for i, a in enumerate(tiles):
-                m = slice(a % 2 * P, (a % 2 + 1) * P)
-                nc.tensor.matmul_mx(out=acc[:, i * cw:(i + 1) * cw], lhsT=w2_codes[a // 2][:, m].bitcast(FP8X4), lhsT_scale=w2_scales[a // 2][:, m],
-                                    rhs=z_codes[:, w0:w0 + cw].bitcast(FP8X4), rhs_scale=z_scales[:, w0:w0 + cw], start=True, stop=True)
-            copy(res, acc[:, 0:len(tiles) * cw])
+        def multiply(copy, res, a, w0, cw, b):
+            acc = bank(b)
+            nc.tensor.matmul_mx(out=acc[:, 0:cw], lhsT=w2_codes[a].bitcast(FP8X4), lhsT_scale=w2_scales[a],
+                                rhs=z_codes[:, w0:w0 + cw].bitcast(FP8X4), rhs_scale=z_scales[:, w0:w0 + cw], start=True, stop=True)
+            copy(res, acc[:, 0:cw])
 
-        def strip(copy, tiles, i, tag):
-            w0, cw = starts[i], CHUNKS[i]
-            res = keep.tile([P, len(tiles) * cw], F32, name=tag, tag=tag, align_bytes=64)
-            multiply(copy, res[:], tiles, w0, cw)
-            nc.sync.dma_start(out_rows[:, tiles[0]:tiles[-1] + 1, w0:w0 + cw], res[:].rearrange("p (a w) -> p a w", a=len(tiles)))
+        def piece(a, w0, cw, copies, banks):
+            res = keep.tile([P, len(copies) * cw], F32, name="res%d_%d" % (a, w0), align_bytes=64)
+            for i, copy in enumerate(copies):
+                multiply(copy, res[:, i * cw:(i + 1) * cw], a, w0 + i * cw, cw, banks[i])
+            nc.sync.dma_start(out_rows[:, a, w0:w0 + len(copies) * cw], res[:])
 
-        quantize_w2(0)
+        on_scalar, on_vector = nc.scalar.copy, nc.vector.tensor_copy
+        convert(4)
+        convert(5)
+        quantize_w2((0,))
+        for b in (6, 7):
+            nc.tensor.matmul_mx(out=bank(b)[:], lhsT=w2_codes[0].bitcast(FP8X4), lhsT_scale=w2_scales[0],
+                                rhs=gw[:].bitcast(FP8X4), rhs_scale=gs[:], start=True, stop=True)
         convert(0)
         convert(1)
+        quantize_w2((1,))
         quantize(0)
         quantize(1)
-        quantize_w2(1)
         convert(2)
         convert(3)
         quantize(2)
         quantize(3)
-        convert(4)
-        for a in range(4):
-            res = keep.tile([P, HALF], F32, name="res0_%d" % a, align_bytes=64)
-            multiply(nc.vector.tensor_copy if a == 3 else nc.scalar.copy, res[:], (a,), 0, HALF)
-            nc.sync.dma_start(out_rows[:, a, 0:HALF], res[:])
         quantize(4)
-        strip(nc.scalar.copy, (0,), 2, "res2_0")
-        strip(nc.scalar.copy, (1,), 2, "res2_1")
-        res = keep.tile([P, 2, HALF], F32, name="res2_2", align_bytes=64)
-        multiply(nc.vector.tensor_copy, res[:, 0, :], (2,), starts[2], HALF)
-        multiply(nc.scalar.copy, res[:, 1, :], (3,), starts[2], HALF)
-        nc.sync.dma_start(out_rows[:, 2:4, starts[2]:starts[3]], res[:])
-        for tiles in ((0, 1), (2, 3)):
-            res = keep.tile([P, len(tiles), BANK], F32, name="rows%d" % tiles[0], align_bytes=64)
-            for i, a in enumerate(tiles):
-                multiply(nc.vector.tensor_copy, res[:, i, 0:HALF], (a,), starts[3], HALF)
-                multiply(nc.scalar.copy, res[:, i, HALF:BANK], (a,), starts[4], HALF)
-            nc.sync.dma_start(out_rows[:, tiles[0]:tiles[-1] + 1, BANK:U], res[:])
+        quantize(5)
+        quantize_w2((2, 3))
+        piece(0, 0, HALF, (on_scalar,), (0,))
+        piece(1, 0, HALF, (on_scalar,), (1,))
+        piece(0, HALF, HALF, (on_scalar,), (2,))
+        piece(1, HALF, HALF, (on_scalar,), (3,))
+        piece(0, BANK, HALF, (on_scalar, on_vector), (4, 5))
+        piece(1, BANK, HALF, (on_scalar, on_vector), (2, 3))
+        piece(2, 0, HALF, (on_scalar, on_vector), (6, 7))
+        piece(2, BANK, HALF, (on_scalar, on_vector), (0, 1))
+        piece(3, 0, HALF, (on_scalar, on_vector, on_scalar, on_vector), (4, 5, 2, 3))

@@ -17,7 +17,7 @@ P = 128
 PACK = 4
 BANK = 512
 HALF = S // 2
-CHUNKS = (128, 128, 128, 128, 256, 256)
+CHUNKS = (128, 128, 256, 128, 128, 256)
 
 
 def tile_picked_pagemix_none_p_kernel(tc, x_words, x_scales, w1, mem, w2, offs, slot, out):
@@ -36,9 +36,9 @@ def tile_picked_pagemix_none_p_kernel(tc, x_words, x_scales, w1, mem, w2, offs, 
         mem_rows = mem.rearrange("(p t) w -> t p w", t=PACK)
         nc.scalar.dma_start(xs[16:32, :].bitcast(I32), x_scales[0].bitcast(I32))
         nc.sync.dma_start(offs_sb[:], offs)
-        nc.sync.dma_start(slot_sb[:], slot)
         nc.sync.dma_start(w1_raw[:], w1.rearrange("(p j) c -> p j c", j=PACK))
         nc.sync.dma_start(xw[:].bitcast(I32), x_words[0].rearrange("p c r -> p (c r)").bitcast(I32))
+        nc.sync.dma_start(slot_sb[:], slot)
 
         for rows in (slice(0, 16), slice(32, 64), slice(64, P)):
             nc.vector.memset(xs[rows, :].bitcast(I32), 0)
@@ -127,7 +127,7 @@ def tile_picked_pagemix_none_p_kernel(tc, x_words, x_scales, w1, mem, w2, offs, 
             if tiles[0] == 0:
                 codes = shared.tile([P, width], U32, name="w2_codes0", tag="page1", align_bytes=64, offset=4096)
             else:
-                codes = keep.tile([P, width], U32, name="w2_codes%d" % tiles[0], tag=("y0_0", "z_grouped5")[tiles[0] - 1], align_bytes=64)
+                codes = keep.tile([P, width], U32, name="w2_codes%d" % tiles[0], tag="y0_0", align_bytes=64)
             scales = keep.tile([P, width], U8, name="w2_scales%d" % tiles[0], align_bytes=64)
             c0 = tiles[0] % 2 * P
             nc.vector.quantize_mx(out=codes[:].bitcast(FP8X4), scales=scales[:], in_=w2_grouped[tiles[0] // 2][:, c0:c0 + width, :].rearrange("p c j -> p (c j)"))
@@ -161,22 +161,22 @@ def tile_picked_pagemix_none_p_kernel(tc, x_words, x_scales, w1, mem, w2, offs, 
                                 rhs=z_codes[:, w0:w0 + cw].bitcast(FP8X4), rhs_scale=z_scales[:, w0:w0 + cw], start=True, stop=True)
             copy(res, acc[:, 0:cw])
 
-        def piece(a, w0, cw, copies, banks):
-            res = keep.tile([P, len(copies) * cw], F32, name="res%d_%d" % (a, w0), align_bytes=64)
+        def piece(tiles, w0, copies, banks):
+            units = len(copies) // len(tiles)
+            res = keep.tile([P, len(tiles), units * HALF], F32, name="res%d_%d" % (tiles[0], w0), align_bytes=64)
             for i, copy in enumerate(copies):
-                multiply(copy, res[:, i * cw:(i + 1) * cw], a, w0 + i * cw, cw, banks[i])
-            nc.sync.dma_start(out_rows[:, a, w0:w0 + len(copies) * cw], res[:])
+                row, col = divmod(i, units)
+                multiply(copy, res[:, row, col * HALF:(col + 1) * HALF], tiles[row], w0 + col * HALF, HALF, banks[i])
+            nc.sync.dma_start(out_rows[:, tiles[0]:tiles[-1] + 1, w0:w0 + units * HALF], res[:])
+            return res
 
         on_scalar, on_vector = nc.scalar.copy, nc.vector.tensor_copy
         convert(4)
         convert(5)
-        quantize_w2((0,))
-        for b in (6, 7):
-            nc.tensor.matmul_mx(out=bank(b)[:], lhsT=w2_codes[0].bitcast(FP8X4), lhsT_scale=w2_scales[0],
-                                rhs=gw[:].bitcast(FP8X4), rhs_scale=gs[:], start=True, stop=True)
+        quantize_w2((0, 1))
         convert(0)
         convert(1)
-        quantize_w2((1,))
+        quantize_w2((2, 3))
         quantize(0)
         quantize(1)
         convert(2)
@@ -185,13 +185,17 @@ def tile_picked_pagemix_none_p_kernel(tc, x_words, x_scales, w1, mem, w2, offs, 
         quantize(3)
         quantize(4)
         quantize(5)
-        quantize_w2((2, 3))
-        piece(0, 0, HALF, (on_scalar,), (0,))
-        piece(1, 0, HALF, (on_scalar,), (1,))
-        piece(0, HALF, HALF, (on_scalar,), (2,))
-        piece(1, HALF, HALF, (on_scalar,), (3,))
-        piece(0, BANK, HALF, (on_scalar, on_vector), (4, 5))
-        piece(1, BANK, HALF, (on_scalar, on_vector), (2, 3))
-        piece(2, 0, HALF, (on_scalar, on_vector), (6, 7))
-        piece(2, BANK, HALF, (on_scalar, on_vector), (0, 1))
-        piece(3, 0, HALF, (on_scalar, on_vector, on_scalar, on_vector), (4, 5, 2, 3))
+        res = keep.tile([P, HALF], F32, name="res0_0", align_bytes=64)
+        multiply(on_scalar, res[:, 0:P], 0, 0, P, 6)
+        multiply(on_scalar, res[:, P:HALF], 0, P, P, 0)
+        nc.sync.dma_start(out_rows[:, 0, 0:HALF], res[:])
+        for a in range(1, 4):
+            piece((a,), 0, (on_scalar,), (a,))
+        piece((0,), HALF, (on_scalar,), (4,))
+        piece((1,), HALF, (on_scalar,), (5,))
+        piece((2, 3), HALF, (on_vector, on_scalar), (6, 7))
+        piece((0, 1), BANK, (on_vector, on_scalar, on_vector, on_scalar), (0, 1, 2, 3))
+        res = keep.tile([P, 2, BANK], F32, name="res_last", align_bytes=64)
+        multiply(on_vector, res[:, 0, :], 2, BANK, BANK, 4)
+        multiply(on_scalar, res[:, 1, :], 3, BANK, BANK, 5)
+        nc.sync.dma_start(out_rows[:, 2:4, BANK:U], res[:])

@@ -17,7 +17,7 @@ P = 128
 PACK = 4
 BANK = 512
 HALF = S // 2
-CHUNKS = (128, 128, 256, 128, 128, 256)
+CHUNKS = (128, 128, 128, 128, 128, 128, 256)
 
 
 def tile_picked_pagemix_none_p_kernel(tc, x_words, x_scales, w1, mem, w2, offs, slot, out):
@@ -147,7 +147,7 @@ def tile_picked_pagemix_none_p_kernel(tc, x_words, x_scales, w1, mem, w2, offs, 
         z_scales = keep.tile([P, U], U8, name="z_scales", align_bytes=64)
 
         def convert(i):
-            copy = nc.scalar.copy if i >= 4 else nc.vector.tensor_copy
+            copy = nc.scalar.copy if i >= 5 else nc.vector.tensor_copy
             copy(z_grouped[i][:, :, 0:2], src01[:, starts[i]:starts[i] + CHUNKS[i], :])
 
         def quantize(i):
@@ -171,20 +171,22 @@ def tile_picked_pagemix_none_p_kernel(tc, x_words, x_scales, w1, mem, w2, offs, 
             return res
 
         on_scalar, on_vector = nc.scalar.copy, nc.vector.tensor_copy
-        convert(4)
         convert(5)
+        convert(6)
         quantize_w2((0, 1))
         convert(0)
         convert(1)
-        quantize_w2((2, 3))
+        convert(2)
         quantize(0)
         quantize(1)
-        convert(2)
         convert(3)
+        quantize_w2((2, 3))
         quantize(2)
         quantize(3)
-        quantize(4)
+        convert(4)
         quantize(5)
+        quantize(4)
+        quantize(6)
         res = keep.tile([P, HALF], F32, name="res0_0", align_bytes=64)
         multiply(on_scalar, res[:, 0:P], 0, 0, P, 6)
         multiply(on_scalar, res[:, P:HALF], 0, P, P, 0)

@@ -17,7 +17,7 @@ P = 128
 PACK = 4
 BANK = 512
 HALF = S // 2
-CHUNKS = (128, 128, 128, 128, 128, 128, 256)
+CHUNKS = (128, 128, 128, 128, 256, 256)
 
 
 def tile_picked_pagemix_none_p_kernel(tc, x_words, x_scales, w1, mem, w2, offs, slot, out):
@@ -34,20 +34,19 @@ def tile_picked_pagemix_none_p_kernel(tc, x_words, x_scales, w1, mem, w2, offs, 
         w1_raw = shared.tile([P, PACK, H], F32, name="w1_raw", align_bytes=64, offset=12288)
 
         mem_rows = mem.rearrange("(p t) w -> t p w", t=PACK)
-        nc.scalar.dma_start(xs[16:32, :].bitcast(I32), x_scales[0].bitcast(I32))
+        nc.scalar.dma_start(xs[112:P, :].bitcast(I32), x_scales[0].bitcast(I32))
         nc.sync.dma_start(offs_sb[:], offs)
         nc.sync.dma_start(w1_raw[:], w1.rearrange("(p j) c -> p j c", j=PACK))
         nc.sync.dma_start(xw[:].bitcast(I32), x_words[0].rearrange("p c r -> p (c r)").bitcast(I32))
         nc.sync.dma_start(slot_sb[:], slot)
 
-        for rows in (slice(0, 16), slice(32, 64), slice(64, P)):
-            nc.vector.memset(xs[rows, :].bitcast(I32), 0)
+        nc.vector.memset(xs[0:112, :].bitcast(I32), 0)
         gs = keep.tile([P, S], U8, name="gs", align_bytes=64)
         nc.vector.memset(gs[:].bitcast(I32), 0)
         picked = keep.tile([P, S], U8, name="picked", align_bytes=64)
         nc.vector.tensor_copy(picked[:], xs[:].indirect(offs_sb[:]))
         for q in range(4):
-            nc.sync.dma_start(gs[32 * q:32 * q + 4, :].bitcast(I32), picked[16 + 4 * q:20 + 4 * q, :].bitcast(I32))
+            nc.sync.dma_start(gs[32 * q:32 * q + 4, :].bitcast(I32), picked[112 + 4 * q:116 + 4 * q, :].bitcast(I32))
 
         page3 = shared.tile([P, U], F32, name="page3", tag="page3", align_bytes=64, offset=0)
         nc.sync.dma_start(page3[:], mem_rows[3])
@@ -146,9 +145,8 @@ def tile_picked_pagemix_none_p_kernel(tc, x_words, x_scales, w1, mem, w2, offs, 
         z_codes = keep.tile([P, U], U32, name="z_codes", align_bytes=64)
         z_scales = keep.tile([P, U], U8, name="z_scales", align_bytes=64)
 
-        def convert(i):
-            copy = nc.scalar.copy if i >= 5 else nc.vector.tensor_copy
-            copy(z_grouped[i][:, :, 0:2], src01[:, starts[i]:starts[i] + CHUNKS[i], :])
+        def convert(copy, i, lo, hi):
+            copy(z_grouped[i][:, lo:hi, 0:2], src01[:, starts[i] + lo:starts[i] + hi, :])
 
         def quantize(i):
             nc.vector.quantize_mx(out=z_codes[:, starts[i]:starts[i] + CHUNKS[i]].bitcast(FP8X4), scales=z_scales[:, starts[i]:starts[i] + CHUNKS[i]], in_=z_grouped[i][:].rearrange("p w j -> p (w j)"))
@@ -171,22 +169,21 @@ def tile_picked_pagemix_none_p_kernel(tc, x_words, x_scales, w1, mem, w2, offs, 
             return res
 
         on_scalar, on_vector = nc.scalar.copy, nc.vector.tensor_copy
-        convert(5)
-        convert(6)
+        convert(on_scalar, 4, P, HALF)
+        convert(on_scalar, 5, 0, HALF)
         quantize_w2((0, 1))
-        convert(0)
-        convert(1)
-        convert(2)
+        convert(on_vector, 0, 0, P)
+        convert(on_vector, 1, 0, P)
+        convert(on_vector, 2, 0, P)
         quantize(0)
         quantize(1)
-        convert(3)
+        convert(on_vector, 3, 0, P)
         quantize_w2((2, 3))
         quantize(2)
         quantize(3)
-        convert(4)
+        convert(on_vector, 4, 0, P)
         quantize(5)
         quantize(4)
-        quantize(6)
         res = keep.tile([P, HALF], F32, name="res0_0", align_bytes=64)
         multiply(on_scalar, res[:, 0:P], 0, 0, P, 6)
         multiply(on_scalar, res[:, P:HALF], 0, P, P, 0)

@@ -17,11 +17,13 @@ P = 128
 PACK = 4
 BANK = 512
 HALF = S // 2
-CHUNKS = (128, 128, 128, 128, 256, 256)
+CHUNKS = (128, 128, 128, 128, 512)
+SPLIT = 640
 
 
 def tile_picked_pagemix_none_p_kernel(tc, x_words, x_scales, w1, mem, w2, offs, slot, out):
     nc = tc.nc
+    on_scalar, on_vector = nc.scalar.copy, nc.vector.tensor_copy
     with ExitStack() as ctx:
         keep = ctx.enter_context(tc.tile_pool(name="keep", bufs=1))
         shared = ctx.enter_context(tc.tile_pool(name="shared", bufs=1))
@@ -33,7 +35,6 @@ def tile_picked_pagemix_none_p_kernel(tc, x_words, x_scales, w1, mem, w2, offs, 
         xs = shared.tile([P, T], U8, name="xs", align_bytes=64, offset=3072)
         w1_raw = shared.tile([P, PACK, H], F32, name="w1_raw", align_bytes=64, offset=12288)
 
-        mem_rows = mem.rearrange("(p t) w -> t p w", t=PACK)
         nc.scalar.dma_start(xs[112:P, :].bitcast(I32), x_scales[0].bitcast(I32))
         nc.sync.dma_start(offs_sb[:], offs)
         nc.sync.dma_start(w1_raw[:], w1.rearrange("(p j) c -> p j c", j=PACK))
@@ -44,19 +45,20 @@ def tile_picked_pagemix_none_p_kernel(tc, x_words, x_scales, w1, mem, w2, offs, 
         gs = keep.tile([P, S], U8, name="gs", align_bytes=64)
         nc.vector.memset(gs[:].bitcast(I32), 0)
         picked = keep.tile([P, S], U8, name="picked", align_bytes=64)
-        nc.vector.tensor_copy(picked[:], xs[:].indirect(offs_sb[:]))
+        on_vector(picked[:], xs[:].indirect(offs_sb[:]))
         for q in range(4):
             nc.sync.dma_start(gs[32 * q:32 * q + 4, :].bitcast(I32), picked[112 + 4 * q:116 + 4 * q, :].bitcast(I32))
 
-        page3 = shared.tile([P, U], F32, name="page3", tag="page3", align_bytes=64, offset=0)
-        nc.sync.dma_start(page3[:], mem_rows[3])
-        page1 = shared.tile([P, U], F32, name="page1", tag="page1", align_bytes=64, offset=4096)
+        mem_rows = mem.rearrange("(p t) w -> t p w", t=PACK)
+        page1 = shared.tile([P, U], F32, name="page1", tag="page1", align_bytes=64, offset=0)
         nc.sync.dma_start(page1[:], mem_rows[1])
+        page3 = shared.tile([P, U], F32, name="page3", tag="page3", align_bytes=64, offset=4096)
+        nc.sync.dma_start(page3[:], mem_rows[3])
 
         w1_src = w1_raw[:].rearrange("p j (m t) -> p m j t", t=PACK)
         w1_codes = {}
         w1_scales = {}
-        for t0, copy in ((2, nc.vector.tensor_copy), (0, nc.scalar.copy)):
+        for t0, copy in ((0, on_vector), (2, on_scalar)):
             grouped = keep.tile([P, 2, P, PACK], BF16, name="w1_grouped%d" % t0, align_bytes=64)
             copy(grouped[:].rearrange("p t m j -> p m j t"), w1_src[:, :, :, t0:t0 + 2])
             codes = keep.tile([P, 2 * P], U32, name="w1_codes%d" % t0, align_bytes=64)
@@ -76,125 +78,108 @@ def tile_picked_pagemix_none_p_kernel(tc, x_words, x_scales, w1, mem, w2, offs, 
         nc.sync.dma_start(page23[:, 0:U], mem_rows[2])
 
         gw = keep.tile([P, S], U32, name="gw", align_bytes=64)
-        for h in range(2):
-            nc.vector.tensor_copy(gw[:, h * HALF:(h + 1) * HALF], xw[:].indirect(offs_sb[:, h * 16:(h + 1) * 16]))
+        for lo, hi in ((0, P), (P, HALF), (HALF, S)):
+            on_vector(gw[:, lo:hi], xw[:].indirect(offs_sb[:, lo // 16:hi // 16]))
 
         def bank(b):
             return psum.tile([P, BANK], F32, name="bank%d" % b, tag="bank%d" % b)
 
+        pieces = [(1, (0, P, HALF)), (3, (0, S)), (2, (0, S)), (0, (0, S)), (1, (HALF, S))]
+        ys = {}
         used = []
-
-        def project(t, cuts):
+        for t, cuts in pieces:
             y = keep.tile([P, cuts[-1] - cuts[0]], F32, name="y%d_%d" % (t, cuts[0]), tag="y%d_%d" % (t, cuts[0]), align_bytes=64)
             for lo, hi in zip(cuts, cuts[1:]):
                 acc = bank(len(used))
                 used.append(lo)
                 nc.tensor.matmul_mx(out=acc[:, 0:hi - lo], lhsT=w1_codes[t].bitcast(FP8X4), lhsT_scale=w1_scales[t],
                                     rhs=gw[:, lo:hi].bitcast(FP8X4), rhs_scale=gs[:, lo:hi], start=True, stop=True)
-                nc.scalar.copy(y[:, lo - cuts[0]:hi - cuts[0]], acc[:, 0:hi - lo])
-            return y
+                on_scalar(y[:, lo - cuts[0]:hi - cuts[0]], acc[:, 0:hi - lo])
+            ys[t, cuts[0], cuts[-1]] = y
 
-        pieces = [(3, (0, 128)), (3, (128, HALF, S)), (1, (0, S)), (2, (0, S)), (0, (0, S))]
-        ys = [project(t, cuts) for t, cuts in pieces]
-
-        def scatter(i, window):
-            t, cuts = pieces[i]
-            nc.vector.tensor_copy(window[:].indirect(slot_sb[:, cuts[0] // 16:cuts[-1] // 16]), ys[i][:])
-
-        scatter(0, page3)
-        scatter(1, page3)
+        def scatter(window, t, lo, hi):
+            on_vector(window[:].indirect(slot_sb[:, lo // 16:hi // 16]), ys[t, lo, hi][:])
 
         w2_grouped = []
 
         def round_w2(h):
-            w2_grouped.append(shared.tile([P, N // 2, PACK], BF16, name="w2_grouped%d" % h, tag=("w2_grouped0", "page3")[h], align_bytes=64, offset=(24576, 0)[h]))
-            nc.scalar.copy(w2_grouped[h][:].rearrange("p (c i) j -> p c j i", i=4), w2_raw[h].rearrange("p j (c i) -> p c j i", i=4))
+            w2_grouped.append(shared.tile([P, N // 2, PACK], BF16, name="w2_grouped%d" % h, tag=("w2_grouped0", "page3")[h], align_bytes=64, offset=(24576, 4096)[h]))
+            on_scalar(w2_grouped[h][:].rearrange("p (c i) j -> p c j i", i=4), w2_raw[h].rearrange("p j (c i) -> p c j i", i=4))
 
+        scatter(page1, 1, 0, HALF)
+        scatter(page3, 3, 0, S)
+        scatter(page1, 1, HALF, S)
         round_w2(0)
-        nc.scalar.copy(page23[:, U:2 * U], page3[:])
+        on_scalar(page23[:, U:2 * U], page3[:])
         round_w2(1)
-
-        scatter(2, page1)
-        nc.scalar.copy(page01[:, U:2 * U], page1[:])
-        scatter(3, page23)
-
-        w2_codes = {}
-        w2_scales = {}
-
-        def quantize_w2(tiles):
-            width = len(tiles) * P
-            if tiles[0] == 0:
-                codes = shared.tile([P, width], U32, name="w2_codes0", tag="page1", align_bytes=64, offset=4096)
-            else:
-                codes = keep.tile([P, width], U32, name="w2_codes%d" % tiles[0], tag="y0_0", align_bytes=64)
-            scales = keep.tile([P, width], U8, name="w2_scales%d" % tiles[0], align_bytes=64)
-            c0 = tiles[0] % 2 * P
-            nc.vector.quantize_mx(out=codes[:].bitcast(FP8X4), scales=scales[:], in_=w2_grouped[tiles[0] // 2][:, c0:c0 + width, :].rearrange("p c j -> p (c j)"))
-            for i, a in enumerate(tiles):
-                w2_codes[a] = codes[:, i * P:(i + 1) * P]
-                w2_scales[a] = scales[:, i * P:(i + 1) * P]
+        scatter(page23, 2, 0, S)
+        on_scalar(page01[:, U:2 * U], page1[:])
 
         starts = [sum(CHUNKS[:i]) for i in range(len(CHUNKS))]
         z_grouped = [keep.tile([P, cw, PACK], BF16, name="z_grouped%d" % i, tag="z_grouped%d" % i, align_bytes=64) for i, cw in enumerate(CHUNKS)]
         src23 = page23[:].rearrange("p (h w) -> p w h", h=2)
         src01 = page01[:].rearrange("p (h w) -> p w h", h=2)
-        for i in range(len(CHUNKS)):
-            nc.scalar.copy(z_grouped[i][:, :, 2:4], src23[:, starts[i]:starts[i] + CHUNKS[i], :])
-        scatter(4, page01)
+        for i, cw in enumerate(CHUNKS):
+            on_scalar(z_grouped[i][:, :, 2:4], src23[:, starts[i]:starts[i] + cw, :])
+        scatter(page01, 0, 0, S)
+
+        w2_codes = {}
+        w2_scales = {}
+
+        def quantize_w2(h):
+            if h == 0:
+                codes = shared.tile([P, 2 * P], U32, name="w2_codes0", tag="page1", align_bytes=64, offset=0)
+            else:
+                codes = keep.tile([P, 2 * P], U32, name="w2_codes1", tag="y0_0", align_bytes=64)
+            scales = keep.tile([P, 2 * P], U8, name="w2_scales%d" % h, align_bytes=64)
+            nc.vector.quantize_mx(out=codes[:].bitcast(FP8X4), scales=scales[:], in_=w2_grouped[h][:].rearrange("p c j -> p (c j)"))
+            for i in range(2):
+                w2_codes[2 * h + i] = codes[:, i * P:(i + 1) * P]
+                w2_scales[2 * h + i] = scales[:, i * P:(i + 1) * P]
 
         z_codes = keep.tile([P, U], U32, name="z_codes", align_bytes=64)
         z_scales = keep.tile([P, U], U8, name="z_scales", align_bytes=64)
 
         def convert(copy, i, lo, hi):
-            copy(z_grouped[i][:, lo:hi, 0:2], src01[:, starts[i] + lo:starts[i] + hi, :])
+            copy(z_grouped[i][:, lo - starts[i]:hi - starts[i], 0:2], src01[:, lo:hi, :])
 
         def quantize(i):
-            nc.vector.quantize_mx(out=z_codes[:, starts[i]:starts[i] + CHUNKS[i]].bitcast(FP8X4), scales=z_scales[:, starts[i]:starts[i] + CHUNKS[i]], in_=z_grouped[i][:].rearrange("p w j -> p (w j)"))
+            cols = slice(starts[i], starts[i] + CHUNKS[i])
+            nc.vector.quantize_mx(out=z_codes[:, cols].bitcast(FP8X4), scales=z_scales[:, cols], in_=z_grouped[i][:].rearrange("p w j -> p (w j)"))
+
+        convert(on_scalar, 4, SPLIT, U)
+        quantize_w2(0)
+        convert(on_vector, 0, 0, 128)
+        convert(on_vector, 1, 128, 256)
+        convert(on_vector, 2, 256, 384)
+        quantize(0)
+        quantize(1)
+        convert(on_vector, 3, 384, 512)
+        quantize_w2(1)
+        quantize(2)
+        convert(on_vector, 4, 512, SPLIT)
+        quantize(3)
+        quantize(4)
 
         out_rows = out.rearrange("(a p) w -> p a w", p=P)
 
-        def multiply(copy, res, a, w0, cw, b):
+        def multiply(copy, res, a, lo, hi, b):
             acc = bank(b)
-            nc.tensor.matmul_mx(out=acc[:, 0:cw], lhsT=w2_codes[a].bitcast(FP8X4), lhsT_scale=w2_scales[a],
-                                rhs=z_codes[:, w0:w0 + cw].bitcast(FP8X4), rhs_scale=z_scales[:, w0:w0 + cw], start=True, stop=True)
-            copy(res, acc[:, 0:cw])
+            nc.tensor.matmul_mx(out=acc[:, 0:hi - lo], lhsT=w2_codes[a].bitcast(FP8X4), lhsT_scale=w2_scales[a],
+                                rhs=z_codes[:, lo:hi].bitcast(FP8X4), rhs_scale=z_scales[:, lo:hi], start=True, stop=True)
+            copy(res, acc[:, 0:hi - lo])
 
-        def piece(tiles, w0, copies, banks):
-            units = len(copies) // len(tiles)
-            res = keep.tile([P, len(tiles), units * HALF], F32, name="res%d_%d" % (tiles[0], w0), align_bytes=64)
-            for i, copy in enumerate(copies):
-                row, col = divmod(i, units)
-                multiply(copy, res[:, row, col * HALF:(col + 1) * HALF], tiles[row], w0 + col * HALF, HALF, banks[i])
-            nc.sync.dma_start(out_rows[:, tiles[0]:tiles[-1] + 1, w0:w0 + units * HALF], res[:])
-            return res
+        def store(a0, a1, lo, hi, passes):
+            res = keep.tile([P, a1 - a0, hi - lo], F32, name="res%d_%d" % (a0, lo), align_bytes=64)
+            for copy, a, c0, c1, b in passes:
+                multiply(copy, res[:, a - a0, c0 - lo:c1 - lo], a, c0, c1, b)
+            nc.sync.dma_start(out_rows[:, a0:a1, lo:hi], res[:])
 
-        on_scalar, on_vector = nc.scalar.copy, nc.vector.tensor_copy
-        convert(on_scalar, 4, P, HALF)
-        convert(on_scalar, 5, 0, HALF)
-        quantize_w2((0, 1))
-        convert(on_vector, 0, 0, P)
-        convert(on_vector, 1, 0, P)
-        convert(on_vector, 2, 0, P)
-        quantize(0)
-        quantize(1)
-        convert(on_vector, 3, 0, P)
-        quantize_w2((2, 3))
-        quantize(2)
-        quantize(3)
-        convert(on_vector, 4, 0, P)
-        quantize(5)
-        quantize(4)
-        res = keep.tile([P, HALF], F32, name="res0_0", align_bytes=64)
-        multiply(on_scalar, res[:, 0:P], 0, 0, P, 6)
-        multiply(on_scalar, res[:, P:HALF], 0, P, P, 0)
-        nc.sync.dma_start(out_rows[:, 0, 0:HALF], res[:])
+        store(0, 1, 0, 256, [(on_scalar, 0, 0, 128, 6), (on_scalar, 0, 128, 256, 0)])
         for a in range(1, 4):
-            piece((a,), 0, (on_scalar,), (a,))
-        piece((0,), HALF, (on_scalar,), (4,))
-        piece((1,), HALF, (on_scalar,), (5,))
-        piece((2, 3), HALF, (on_vector, on_scalar), (6, 7))
-        piece((0, 1), BANK, (on_vector, on_scalar, on_vector, on_scalar), (0, 1, 2, 3))
-        res = keep.tile([P, 2, BANK], F32, name="res_last", align_bytes=64)
-        multiply(on_vector, res[:, 0, :], 2, BANK, BANK, 4)
-        multiply(on_scalar, res[:, 1, :], 3, BANK, BANK, 5)
-        nc.sync.dma_start(out_rows[:, 2:4, BANK:U], res[:])
+            store(a, a + 1, 0, 256, [(on_scalar, a, 0, 256, a)])
+        store(0, 1, 256, 512, [(on_scalar, 0, 256, 512, 4)])
+        store(1, 2, 256, 512, [(on_scalar, 1, 256, 512, 5)])
+        store(2, 4, 256, 512, [(on_vector, 2, 256, 512, 6), (on_scalar, 3, 256, 512, 7)])
+        store(0, 2, 512, U, [(on_vector, 0, 512, 768, 0), (on_scalar, 0, 768, U, 1), (on_vector, 1, 512, 768, 2), (on_scalar, 1, 768, U, 3)])
+        store(2, 4, 512, U, [(on_vector, 2, 512, U, 4), (on_scalar, 3, 512, U, 5)])

@@ -19,6 +19,7 @@ BANK = 512
 HALF = S // 2
 CHUNKS = (128, 128, 128, 128, 512)
 SPLIT = 640
+FIRST = 192
 
 
 def tile_picked_pagemix_none_p_kernel(tc, x_words, x_scales, w1, mem, w2, offs, slot, out):
@@ -58,15 +59,15 @@ def tile_picked_pagemix_none_p_kernel(tc, x_words, x_scales, w1, mem, w2, offs, 
         w1_src = w1_raw[:].rearrange("p j (m t) -> p m j t", t=PACK)
         w1_codes = {}
         w1_scales = {}
-        for t0, copy in ((0, on_vector), (2, on_scalar)):
+        for t0, copy in ((1, on_vector), (0, on_scalar)):
             grouped = keep.tile([P, 2, P, PACK], BF16, name="w1_grouped%d" % t0, align_bytes=64)
-            copy(grouped[:].rearrange("p t m j -> p m j t"), w1_src[:, :, :, t0:t0 + 2])
+            copy(grouped[:].rearrange("p t m j -> p m j t"), w1_src[:, :, :, t0:PACK:2])
             codes = keep.tile([P, 2 * P], U32, name="w1_codes%d" % t0, align_bytes=64)
             scales = keep.tile([P, 2 * P], U8, name="w1_scales%d" % t0, align_bytes=64)
             nc.vector.quantize_mx(out=codes[:].bitcast(FP8X4), scales=scales[:], in_=grouped[:].rearrange("p t m j -> p (t m j)"))
             for i in range(2):
-                w1_codes[t0 + i] = codes[:, i * P:(i + 1) * P]
-                w1_scales[t0 + i] = scales[:, i * P:(i + 1) * P]
+                w1_codes[t0 + 2 * i] = codes[:, i * P:(i + 1) * P]
+                w1_scales[t0 + 2 * i] = scales[:, i * P:(i + 1) * P]
 
         page23 = shared.tile([P, 2 * U], F32, name="page23", align_bytes=64, offset=8192)
         page01 = shared.tile([P, 2 * U], F32, name="page01", align_bytes=64, offset=16384)
@@ -78,24 +79,26 @@ def tile_picked_pagemix_none_p_kernel(tc, x_words, x_scales, w1, mem, w2, offs, 
         nc.sync.dma_start(page23[:, 0:U], mem_rows[2])
 
         gw = keep.tile([P, S], U32, name="gw", align_bytes=64)
-        for lo, hi in ((0, P), (P, HALF), (HALF, S)):
+        for lo, hi in ((0, FIRST), (FIRST, S)):
             on_vector(gw[:, lo:hi], xw[:].indirect(offs_sb[:, lo // 16:hi // 16]))
 
         def bank(b):
             return psum.tile([P, BANK], F32, name="bank%d" % b, tag="bank%d" % b)
 
-        pieces = [(1, (0, P, HALF)), (3, (0, S)), (2, (0, S)), (0, (0, S)), (1, (HALF, S))]
+        pieces = [(1, ((0, P, FIRST),)), (3, ((0, HALF), (HALF, S))), (2, ((0, S),)), (0, ((0, S),)), (1, ((FIRST, FIRST + HALF, S),))]
         ys = {}
         used = []
-        for t, cuts in pieces:
-            y = keep.tile([P, cuts[-1] - cuts[0]], F32, name="y%d_%d" % (t, cuts[0]), tag="y%d_%d" % (t, cuts[0]), align_bytes=64)
-            for lo, hi in zip(cuts, cuts[1:]):
+        for t, groups in pieces:
+            first, last = groups[0][0], groups[-1][-1]
+            y = keep.tile([P, last - first], F32, name="y%d_%d" % (t, first), tag="y%d_%d" % (t, first), align_bytes=64)
+            for cuts in groups:
                 acc = bank(len(used))
-                used.append(lo)
-                nc.tensor.matmul_mx(out=acc[:, 0:hi - lo], lhsT=w1_codes[t].bitcast(FP8X4), lhsT_scale=w1_scales[t],
-                                    rhs=gw[:, lo:hi].bitcast(FP8X4), rhs_scale=gs[:, lo:hi], start=True, stop=True)
-                on_scalar(y[:, lo - cuts[0]:hi - cuts[0]], acc[:, 0:hi - lo])
-            ys[t, cuts[0], cuts[-1]] = y
+                used.append(t)
+                for lo, hi in zip(cuts, cuts[1:]):
+                    nc.tensor.matmul_mx(out=acc[:, lo - cuts[0]:hi - cuts[0]], lhsT=w1_codes[t].bitcast(FP8X4), lhsT_scale=w1_scales[t],
+                                        rhs=gw[:, lo:hi].bitcast(FP8X4), rhs_scale=gs[:, lo:hi], start=True, stop=True)
+                on_scalar(y[:, cuts[0] - first:cuts[-1] - first], acc[:, 0:cuts[-1] - cuts[0]])
+            ys[t, first, last] = y
 
         def scatter(window, t, lo, hi):
             on_vector(window[:].indirect(slot_sb[:, lo // 16:hi // 16]), ys[t, lo, hi][:])
@@ -106,9 +109,9 @@ def tile_picked_pagemix_none_p_kernel(tc, x_words, x_scales, w1, mem, w2, offs, 
             w2_grouped.append(shared.tile([P, N // 2, PACK], BF16, name="w2_grouped%d" % h, tag=("w2_grouped0", "page3")[h], align_bytes=64, offset=(24576, 4096)[h]))
             on_scalar(w2_grouped[h][:].rearrange("p (c i) j -> p c j i", i=4), w2_raw[h].rearrange("p j (c i) -> p c j i", i=4))
 
-        scatter(page1, 1, 0, HALF)
+        scatter(page1, 1, 0, FIRST)
         scatter(page3, 3, 0, S)
-        scatter(page1, 1, HALF, S)
+        scatter(page1, 1, FIRST, S)
         round_w2(0)
         on_scalar(page23[:, U:2 * U], page3[:])
         round_w2(1)

@@ -158,31 +158,34 @@ def tile_picked_pagemix_none_p_kernel(tc, x_words, x_scales, w1, mem, w2, offs, 
         quantize(0)
         quantize(1)
         convert(on_vector, 3, 384, 512)
-        quantize_w2(1)
         quantize(2)
         convert(on_vector, 4, 512, SPLIT)
         quantize(3)
+        quantize_w2(1)
         quantize(4)
 
         out_rows = out.rearrange("(a p) w -> p a w", p=P)
 
-        def multiply(copy, res, a, lo, hi, b):
+        def multiply(copy, res, a, cuts, b):
             acc = bank(b)
-            nc.tensor.matmul_mx(out=acc[:, 0:hi - lo], lhsT=w2_codes[a].bitcast(FP8X4), lhsT_scale=w2_scales[a],
-                                rhs=z_codes[:, lo:hi].bitcast(FP8X4), rhs_scale=z_scales[:, lo:hi], start=True, stop=True)
-            copy(res, acc[:, 0:hi - lo])
+            for lo, hi in zip(cuts, cuts[1:]):
+                nc.tensor.matmul_mx(out=acc[:, lo - cuts[0]:hi - cuts[0]], lhsT=w2_codes[a].bitcast(FP8X4), lhsT_scale=w2_scales[a],
+                                    rhs=z_codes[:, lo:hi].bitcast(FP8X4), rhs_scale=z_scales[:, lo:hi], start=True, stop=True)
+            copy(res, acc[:, 0:cuts[-1] - cuts[0]])
 
-        def store(a0, a1, lo, hi, passes):
-            res = keep.tile([P, a1 - a0, hi - lo], F32, name="res%d_%d" % (a0, lo), align_bytes=64)
-            for copy, a, c0, c1, b in passes:
-                multiply(copy, res[:, a - a0, c0 - lo:c1 - lo], a, c0, c1, b)
-            nc.sync.dma_start(out_rows[:, a0:a1, lo:hi], res[:])
+        def store(a, parts):
+            lo, hi = parts[0][1][0], parts[-1][1][-1]
+            res = keep.tile([P, hi - lo], F32, name="res%d_%d" % (a, lo), align_bytes=64)
+            for copy, cuts, b in parts:
+                multiply(copy, res[:, cuts[0] - lo:cuts[-1] - lo], a, cuts, b)
+            nc.sync.dma_start(out_rows[:, a, lo:hi], res[:])
 
-        store(0, 1, 0, 256, [(on_scalar, 0, 0, 128, 6), (on_scalar, 0, 128, 256, 0)])
-        for a in range(1, 4):
-            store(a, a + 1, 0, 256, [(on_scalar, a, 0, 256, a)])
-        store(0, 1, 256, 512, [(on_scalar, 0, 256, 512, 4)])
-        store(1, 2, 256, 512, [(on_scalar, 1, 256, 512, 5)])
-        store(2, 4, 256, 512, [(on_vector, 2, 256, 512, 6), (on_scalar, 3, 256, 512, 7)])
-        store(0, 2, 512, U, [(on_vector, 0, 512, 768, 0), (on_scalar, 0, 768, U, 1), (on_vector, 1, 512, 768, 2), (on_scalar, 1, 768, U, 3)])
-        store(2, 4, 512, U, [(on_vector, 2, 512, U, 4), (on_scalar, 3, 512, U, 5)])
+        store(0, [(on_scalar, (0, 128), 6), (on_scalar, (128, 256), 0)])
+        store(1, [(on_scalar, (0, 256), 1)])
+        store(0, [(on_scalar, (256, 384, 512), 2)])
+        store(1, [(on_scalar, (256, 384, 512), 3)])
+        store(2, [(on_scalar, (0, 256), 4), (on_vector, (256, 512), 6)])
+        store(0, [(on_scalar, (512, 768), 7), (on_vector, (768, U), 5)])
+        store(1, [(on_scalar, (512, 768), 0), (on_vector, (768, U), 1)])
+        store(2, [(on_scalar, (512, U), 2)])
+        store(3, [(on_vector, (0, 512), 7), (on_scalar, (512, U), 4)])

@@ -33,8 +33,8 @@ def tile_picked_pagemix_none_p_kernel(tc, x_words, x_scales, w1, mem, w2, offs, 
         offs_sb = keep.tile([P, S // 16], U16, name="offs_sb")
         slot_sb = keep.tile([P, S // 16], U16, name="slot_sb")
         xw = keep.tile([P, T], U32, name="xw", align_bytes=64)
-        xs = shared.tile([P, T], U8, name="xs", align_bytes=64, offset=3072)
-        w1_raw = shared.tile([P, PACK, H], F32, name="w1_raw", align_bytes=64, offset=12288)
+        xs = shared.tile([P, T], U8, name="xs", align_bytes=64, offset=4032)
+        w1_raw = shared.tile([P, PACK, H], F32, name="w1_raw", align_bytes=64, offset=14336)
 
         nc.scalar.dma_start(xs[112:P, :].bitcast(I32), x_scales[0].bitcast(I32))
         nc.sync.dma_start(offs_sb[:], offs)
@@ -43,17 +43,16 @@ def tile_picked_pagemix_none_p_kernel(tc, x_words, x_scales, w1, mem, w2, offs, 
         nc.sync.dma_start(slot_sb[:], slot)
 
         nc.vector.memset(xs[0:112, :].bitcast(I32), 0)
-        gs = keep.tile([P, S], U8, name="gs", align_bytes=64)
-        nc.vector.memset(gs[:].bitcast(I32), 0)
         picked = keep.tile([P, S], U8, name="picked", align_bytes=64)
         on_vector(picked[:], xs[:].indirect(offs_sb[:]))
+        gs = shared.tile([P, S], U8, name="gs", align_bytes=64, offset=4096)
         for q in range(4):
             nc.sync.dma_start(gs[32 * q:32 * q + 4, :].bitcast(I32), picked[112 + 4 * q:116 + 4 * q, :].bitcast(I32))
 
         mem_rows = mem.rearrange("(p t) w -> t p w", t=PACK)
         page1 = shared.tile([P, U], F32, name="page1", tag="page1", align_bytes=64, offset=0)
         nc.sync.dma_start(page1[:], mem_rows[1])
-        page3 = shared.tile([P, U], F32, name="page3", tag="page3", align_bytes=64, offset=4096)
+        page3 = shared.tile([P, U], F32, name="page3", tag="page3", align_bytes=64, offset=6016)
         nc.sync.dma_start(page3[:], mem_rows[3])
 
         w1_src = w1_raw[:].rearrange("p j (m t) -> p m j t", t=PACK)
@@ -69,8 +68,8 @@ def tile_picked_pagemix_none_p_kernel(tc, x_words, x_scales, w1, mem, w2, offs, 
                 w1_codes[t0 + 2 * i] = codes[:, i * P:(i + 1) * P]
                 w1_scales[t0 + 2 * i] = scales[:, i * P:(i + 1) * P]
 
-        page23 = shared.tile([P, 2 * U], F32, name="page23", align_bytes=64, offset=8192)
-        page01 = shared.tile([P, 2 * U], F32, name="page01", align_bytes=64, offset=16384)
+        page23 = shared.tile([P, 2 * U], F32, name="page23", align_bytes=64, offset=10240)
+        page01 = shared.tile([P, 2 * U], F32, name="page01", align_bytes=64, offset=18432)
         w2_rows = w2.rearrange("(p j) c -> p j c", j=PACK)
         w2_raw = [page[:, U:2 * U].rearrange("p (j c) -> p j c", j=PACK) for page in (page23, page01)]
         for h in range(2):
@@ -106,7 +105,7 @@ def tile_picked_pagemix_none_p_kernel(tc, x_words, x_scales, w1, mem, w2, offs, 
         w2_grouped = []
 
         def round_w2(h):
-            w2_grouped.append(shared.tile([P, N // 2, PACK], BF16, name="w2_grouped%d" % h, tag=("w2_grouped0", "page3")[h], align_bytes=64, offset=(24576, 4096)[h]))
+            w2_grouped.append(shared.tile([P, N // 2, PACK], BF16, name="w2_grouped%d" % h, tag=("w2_grouped0", "page3")[h], align_bytes=64, offset=(26624, 6016)[h]))
             on_scalar(w2_grouped[h][:].rearrange("p (c i) j -> p c j i", i=4), w2_raw[h].rearrange("p j (c i) -> p c j i", i=4))
 
         scatter(page1, 1, 0, FIRST)

@@ -84,7 +84,7 @@ def tile_picked_pagemix_none_p_kernel(tc, x_words, x_scales, w1, mem, w2, offs, 
         def bank(b):
             return psum.tile([P, BANK], F32, name="bank%d" % b, tag="bank%d" % b)
 
-        pieces = [(1, ((0, P, FIRST),)), (3, ((0, HALF), (HALF, S))), (2, ((0, S),)), (0, ((0, S),)), (1, ((FIRST, FIRST + HALF, S),))]
+        pieces = [(1, ((0, P), (P, FIRST))), (3, ((0, P), (P, P + HALF), (P + HALF, S))), (2, ((0, S),)), (0, ((0, S),)), (1, ((FIRST, FIRST + HALF, S),))]
         ys = {}
         used = []
         for t, groups in pieces:
@@ -165,26 +165,31 @@ def tile_picked_pagemix_none_p_kernel(tc, x_words, x_scales, w1, mem, w2, offs, 
 
         out_rows = out.rearrange("(a p) w -> p a w", p=P)
 
-        def multiply(copy, res, a, cuts, b):
+        def multiply(copy, res, b, passes):
             acc = bank(b)
-            for lo, hi in zip(cuts, cuts[1:]):
-                nc.tensor.matmul_mx(out=acc[:, lo - cuts[0]:hi - cuts[0]], lhsT=w2_codes[a].bitcast(FP8X4), lhsT_scale=w2_scales[a],
+            at = 0
+            for a, lo, hi in passes:
+                nc.tensor.matmul_mx(out=acc[:, at:at + hi - lo], lhsT=w2_codes[a].bitcast(FP8X4), lhsT_scale=w2_scales[a],
                                     rhs=z_codes[:, lo:hi].bitcast(FP8X4), rhs_scale=z_scales[:, lo:hi], start=True, stop=True)
-            copy(res, acc[:, 0:cuts[-1] - cuts[0]])
+                at += hi - lo
+            copy(res, acc[:, 0:at] if len(passes) == 1 else acc[:, 0:at].rearrange("p (a w) -> p a w", a=len(passes)))
 
         def store(a, parts):
-            lo, hi = parts[0][1][0], parts[-1][1][-1]
+            lo, hi = parts[0][1], parts[-1][2]
             res = keep.tile([P, hi - lo], F32, name="res%d_%d" % (a, lo), align_bytes=64)
-            for copy, cuts, b in parts:
-                multiply(copy, res[:, cuts[0] - lo:cuts[-1] - lo], a, cuts, b)
+            for copy, first, last, b in parts:
+                multiply(copy, res[:, first - lo:last - lo], b, [(a, first, last)])
             nc.sync.dma_start(out_rows[:, a, lo:hi], res[:])
 
-        store(0, [(on_scalar, (0, 128), 6), (on_scalar, (128, 256), 0)])
-        store(1, [(on_scalar, (0, 256), 1)])
-        store(0, [(on_scalar, (256, 384, 512), 2)])
-        store(1, [(on_scalar, (256, 384, 512), 3)])
-        store(2, [(on_scalar, (0, 256), 4), (on_vector, (256, 512), 6)])
-        store(0, [(on_scalar, (512, 768), 7), (on_vector, (768, U), 5)])
-        store(1, [(on_scalar, (512, 768), 0), (on_vector, (768, U), 1)])
-        store(2, [(on_scalar, (512, U), 2)])
-        store(3, [(on_vector, (0, 512), 7), (on_scalar, (512, U), 4)])
+        store(0, [(on_scalar, 0, 128, 6), (on_scalar, 128, 256, 0)])
+        store(1, [(on_scalar, 0, 256, 1)])
+        second = keep.tile([P, 2, 256], F32, name="second", align_bytes=64)
+        multiply(on_scalar, second[:, :, 0:128], 2, [(0, 256, 384), (1, 256, 384)])
+        for a in range(2):
+            multiply(on_scalar, second[:, a, 128:256], 3 + a, [(a, 384, 512)])
+            nc.sync.dma_start(out_rows[:, a, 256:512], second[:, a, :])
+        store(2, [(on_scalar, 0, 256, 7), (on_scalar, 256, 384, 5), (on_vector, 384, 512, 6)])
+        store(0, [(on_scalar, 512, 768, 0), (on_vector, 768, U, 1)])
+        store(1, [(on_scalar, 512, 768, 2), (on_vector, 768, U, 3)])
+        store(2, [(on_scalar, 512, U, 4)])
+        store(3, [(on_vector, 0, 512, 7), (on_scalar, 512, U, 5)])

@@ -165,31 +165,26 @@ def tile_picked_pagemix_none_p_kernel(tc, x_words, x_scales, w1, mem, w2, offs, 
 
         out_rows = out.rearrange("(a p) w -> p a w", p=P)
 
-        def multiply(copy, res, b, passes):
+        def multiply(copy, res, a, cuts, b):
             acc = bank(b)
-            at = 0
-            for a, lo, hi in passes:
-                nc.tensor.matmul_mx(out=acc[:, at:at + hi - lo], lhsT=w2_codes[a].bitcast(FP8X4), lhsT_scale=w2_scales[a],
+            for lo, hi in zip(cuts, cuts[1:]):
+                nc.tensor.matmul_mx(out=acc[:, lo - cuts[0]:hi - cuts[0]], lhsT=w2_codes[a].bitcast(FP8X4), lhsT_scale=w2_scales[a],
                                     rhs=z_codes[:, lo:hi].bitcast(FP8X4), rhs_scale=z_scales[:, lo:hi], start=True, stop=True)
-                at += hi - lo
-            copy(res, acc[:, 0:at] if len(passes) == 1 else acc[:, 0:at].rearrange("p (a w) -> p a w", a=len(passes)))
+            copy(res, acc[:, 0:cuts[-1] - cuts[0]])
 
-        def store(a, parts):
-            lo, hi = parts[0][1], parts[-1][2]
-            res = keep.tile([P, hi - lo], F32, name="res%d_%d" % (a, lo), align_bytes=64)
-            for copy, first, last, b in parts:
-                multiply(copy, res[:, first - lo:last - lo], b, [(a, first, last)])
-            nc.sync.dma_start(out_rows[:, a, lo:hi], res[:])
+        def store(parts):
+            a0, a1 = parts[0][1], parts[-1][1] + 1
+            lo, hi = parts[0][2][0], parts[-1][2][-1]
+            res = keep.tile([P, a1 - a0, hi - lo], F32, name="res%d_%d" % (a0, lo), align_bytes=64)
+            for copy, a, cuts, b in parts:
+                multiply(copy, res[:, a - a0, cuts[0] - lo:cuts[-1] - lo], a, cuts, b)
+            nc.sync.dma_start(out_rows[:, a0:a1, lo:hi], res[:])
 
-        store(0, [(on_scalar, 0, 128, 6), (on_scalar, 128, 256, 0)])
-        store(1, [(on_scalar, 0, 256, 1)])
-        second = keep.tile([P, 2, 256], F32, name="second", align_bytes=64)
-        multiply(on_scalar, second[:, :, 0:128], 2, [(0, 256, 384), (1, 256, 384)])
-        for a in range(2):
-            multiply(on_scalar, second[:, a, 128:256], 3 + a, [(a, 384, 512)])
-            nc.sync.dma_start(out_rows[:, a, 256:512], second[:, a, :])
-        store(2, [(on_scalar, 0, 256, 7), (on_scalar, 256, 384, 5), (on_vector, 384, 512, 6)])
-        store(0, [(on_scalar, 512, 768, 0), (on_vector, 768, U, 1)])
-        store(1, [(on_scalar, 512, 768, 2), (on_vector, 768, U, 3)])
-        store(2, [(on_scalar, 512, U, 4)])
-        store(3, [(on_vector, 0, 512, 7), (on_scalar, 512, U, 5)])
+        store([(on_scalar, 0, (0, 128), 6), (on_scalar, 0, (128, 256), 0)])
+        store([(on_scalar, 1, (0, 256), 1)])
+        store([(on_scalar, 0, (256, 384), 2), (on_scalar, 0, (384, 512), 3)])
+        store([(on_scalar, 1, (256, 384, 512), 4)])
+        store([(on_scalar, 2, (0, 256), 7), (on_scalar, 2, (256, 384), 5), (on_vector, 2, (384, 512), 6)])
+        store([(on_scalar, 3, (0, 256), 0), (on_vector, 3, (256, 512), 1)])
+        store([(on_scalar, 0, (512, 768), 2), (on_vector, 0, (768, U), 3), (on_scalar, 1, (512, 768), 4), (on_vector, 1, (768, U), 7)])
+        store([(on_scalar, 2, (512, U), 5), (on_vector, 3, (512, U), 0)])

@@ -127,6 +127,7 @@ def tile_picked_pagemix_none_p_kernel(tc, x_words, x_scales, w1, mem, w2, offs, 
 
         w2_codes = {}
         w2_scales = {}
+        w2_half = {}
 
         def quantize_w2(h):
             if h == 0:
@@ -135,6 +136,7 @@ def tile_picked_pagemix_none_p_kernel(tc, x_words, x_scales, w1, mem, w2, offs, 
                 codes = keep.tile([P, 2 * P], U32, name="w2_codes1", tag="y0_0", align_bytes=64)
             scales = keep.tile([P, 2 * P], U8, name="w2_scales%d" % h, align_bytes=64)
             nc.vector.quantize_mx(out=codes[:].bitcast(FP8X4), scales=scales[:], in_=w2_grouped[h][:].rearrange("p c j -> p (c j)"))
+            w2_half[h] = codes, scales
             for i in range(2):
                 w2_codes[2 * h + i] = codes[:, i * P:(i + 1) * P]
                 w2_scales[2 * h + i] = scales[:, i * P:(i + 1) * P]
@@ -179,6 +181,11 @@ def tile_picked_pagemix_none_p_kernel(tc, x_words, x_scales, w1, mem, w2, offs, 
             for copy, a, cuts, b in parts:
                 multiply(copy, res[:, a - a0, cuts[0] - lo:cuts[-1] - lo], a, cuts, b)
             nc.sync.dma_start(out_rows[:, a0:a1, lo:hi], res[:])
+
+        idle = bank(5)
+        for i in range(2):
+            nc.tensor.matmul_mx(out=idle[:, i * 2 * P:(i + 1) * 2 * P], lhsT=w2_codes[i].bitcast(FP8X4), lhsT_scale=w2_scales[i],
+                                rhs=w2_half[0][0][:].bitcast(FP8X4), rhs_scale=w2_half[0][1][:], start=True, stop=True)
 
         store([(on_scalar, 0, (0, 128), 6), (on_scalar, 0, (128, 256), 0)])
         store([(on_scalar, 1, (0, 256), 1)])

@@ -33,8 +33,8 @@ def tile_picked_pagemix_none_p_kernel(tc, x_words, x_scales, w1, mem, w2, offs, 
         offs_sb = keep.tile([P, S // 16], U16, name="offs_sb")
         slot_sb = keep.tile([P, S // 16], U16, name="slot_sb")
         xw = keep.tile([P, T], U32, name="xw", align_bytes=64)
-        xs = shared.tile([P, T], U8, name="xs", align_bytes=64, offset=4032)
-        w1_raw = shared.tile([P, PACK, H], F32, name="w1_raw", align_bytes=64, offset=14336)
+        xs = shared.tile([P, T], U8, name="xs", align_bytes=64, offset=8128)
+        w1_raw = shared.tile([P, PACK, H], F32, name="w1_raw", align_bytes=64, offset=18432)
 
         nc.scalar.dma_start(xs[112:P, :].bitcast(I32), x_scales[0].bitcast(I32))
         nc.sync.dma_start(offs_sb[:], offs)
@@ -45,14 +45,14 @@ def tile_picked_pagemix_none_p_kernel(tc, x_words, x_scales, w1, mem, w2, offs, 
         nc.vector.memset(xs[0:112, :].bitcast(I32), 0)
         picked = keep.tile([P, S], U8, name="picked", align_bytes=64)
         on_vector(picked[:], xs[:].indirect(offs_sb[:]))
-        gs = shared.tile([P, S], U8, name="gs", align_bytes=64, offset=4096)
+        gs = shared.tile([P, S], U8, name="gs", align_bytes=64, offset=8704)
         for q in range(4):
             nc.sync.dma_start(gs[32 * q:32 * q + 4, :].bitcast(I32), picked[112 + 4 * q:116 + 4 * q, :].bitcast(I32))
 
         mem_rows = mem.rearrange("(p t) w -> t p w", t=PACK)
-        page1 = shared.tile([P, U], F32, name="page1", tag="page1", align_bytes=64, offset=0)
+        page1 = shared.tile([P, U], F32, name="page1", tag="page1", align_bytes=64, offset=4096)
         nc.sync.dma_start(page1[:], mem_rows[1])
-        page3 = shared.tile([P, U], F32, name="page3", tag="page3", align_bytes=64, offset=6016)
+        page3 = shared.tile([P, U], F32, name="page3", tag="page3", align_bytes=64, offset=10112)
         nc.sync.dma_start(page3[:], mem_rows[3])
 
         w1_src = w1_raw[:].rearrange("p j (m t) -> p m j t", t=PACK)
@@ -68,14 +68,13 @@ def tile_picked_pagemix_none_p_kernel(tc, x_words, x_scales, w1, mem, w2, offs, 
                 w1_codes[t0 + 2 * i] = codes[:, i * P:(i + 1) * P]
                 w1_scales[t0 + 2 * i] = scales[:, i * P:(i + 1) * P]
 
-        page23 = shared.tile([P, 2 * U], F32, name="page23", align_bytes=64, offset=10240)
-        page01 = shared.tile([P, 2 * U], F32, name="page01", align_bytes=64, offset=18432)
+        page23 = shared.tile([P, 2 * U], F32, name="page23", align_bytes=64, offset=14336)
+        page01 = shared.tile([P, 2 * U], F32, name="page01", align_bytes=64, offset=22528)
         w2_rows = w2.rearrange("(p j) c -> p j c", j=PACK)
         w2_raw = [page[:, U:2 * U].rearrange("p (j c) -> p j c", j=PACK) for page in (page23, page01)]
-        for h in range(2):
+        for h, (page, t) in enumerate(((page23, 2), (page01, 0))):
             nc.sync.dma_start(w2_raw[h], w2_rows[:, :, h * N // 2:(h + 1) * N // 2])
-        nc.sync.dma_start(page01[:, 0:U], mem_rows[0])
-        nc.sync.dma_start(page23[:, 0:U], mem_rows[2])
+            nc.sync.dma_start(page[:, 0:U], mem_rows[t])
 
         gw = keep.tile([P, S], U32, name="gw", align_bytes=64)
         for lo, hi in ((0, FIRST), (FIRST, S)):
@@ -105,7 +104,7 @@ def tile_picked_pagemix_none_p_kernel(tc, x_words, x_scales, w1, mem, w2, offs, 
         w2_grouped = []
 
         def round_w2(h):
-            w2_grouped.append(shared.tile([P, N // 2, PACK], BF16, name="w2_grouped%d" % h, tag=("w2_grouped0", "page3")[h], align_bytes=64, offset=(26624, 6016)[h]))
+            w2_grouped.append(shared.tile([P, N // 2, PACK], BF16, name="w2_grouped%d" % h, tag=("w2_grouped0", "page3")[h], align_bytes=64, offset=(30720, 10112)[h]))
             on_scalar(w2_grouped[h][:].rearrange("p (c i) j -> p c j i", i=4), w2_raw[h].rearrange("p j (c i) -> p c j i", i=4))
 
         scatter(page1, 1, 0, FIRST)
@@ -118,7 +117,7 @@ def tile_picked_pagemix_none_p_kernel(tc, x_words, x_scales, w1, mem, w2, offs, 
         on_scalar(page01[:, U:2 * U], page1[:])
 
         starts = [sum(CHUNKS[:i]) for i in range(len(CHUNKS))]
-        z_grouped = [keep.tile([P, cw, PACK], BF16, name="z_grouped%d" % i, tag="z_grouped%d" % i, align_bytes=64) for i, cw in enumerate(CHUNKS)]
+        z_grouped = [shared.tile([P, cw, PACK], BF16, name="z_grouped%d" % i, align_bytes=64, offset=(4160, 5184, 6208, 7488, 64)[i]) for i, cw in enumerate(CHUNKS)]
         src23 = page23[:].rearrange("p (h w) -> p w h", h=2)
         src01 = page01[:].rearrange("p (h w) -> p w h", h=2)
         for i, cw in enumerate(CHUNKS):
@@ -131,10 +130,11 @@ def tile_picked_pagemix_none_p_kernel(tc, x_words, x_scales, w1, mem, w2, offs, 
 
         def quantize_w2(h):
             if h == 0:
-                codes = shared.tile([P, 2 * P], U32, name="w2_codes0", tag="page1", align_bytes=64, offset=0)
+                codes = keep.tile([P, 2 * P], U32, name="w2_codes0", align_bytes=64)
+                scales = shared.tile([P, 2 * P], U8, name="w2_scales0", align_bytes=64, offset=7232)
             else:
                 codes = keep.tile([P, 2 * P], U32, name="w2_codes1", tag="y0_0", align_bytes=64)
-            scales = keep.tile([P, 2 * P], U8, name="w2_scales%d" % h, align_bytes=64)
+                scales = keep.tile([P, 2 * P], U8, name="w2_scales1", align_bytes=64)
             nc.vector.quantize_mx(out=codes[:].bitcast(FP8X4), scales=scales[:], in_=w2_grouped[h][:].rearrange("p c j -> p (c j)"))
             w2_half[h] = codes, scales
             for i in range(2):

@@ -12,14 +12,15 @@ U32 = mybir.dt.uint32
 U16 = mybir.dt.uint16
 U8 = mybir.dt.uint8
 FP8X4 = mybir.dt.float8_e4m3fn_x4
+COPY = mybir.ActivationFunctionType.Copy
 
 P = 128
 PACK = 4
 BANK = 512
 HALF = S // 2
-CHUNKS = (128, 128, 128, 128, 512)
-SPLIT = 640
-FIRST = 192
+CHUNKS = (128, 128, 256, 256, 256)
+HEAD = 256
+ALIGN = 256
 
 
 def tile_picked_pagemix_none_p_kernel(tc, x_words, x_scales, w1, mem, w2, offs, slot, out):
@@ -32,9 +33,9 @@ def tile_picked_pagemix_none_p_kernel(tc, x_words, x_scales, w1, mem, w2, offs, 
 
         offs_sb = keep.tile([P, S // 16], U16, name="offs_sb")
         slot_sb = keep.tile([P, S // 16], U16, name="slot_sb")
-        xw = keep.tile([P, T], U32, name="xw", align_bytes=64)
-        xs = shared.tile([P, T], U8, name="xs", align_bytes=64, offset=8128)
-        w1_raw = shared.tile([P, PACK, H], F32, name="w1_raw", align_bytes=64, offset=18432)
+        xw = keep.tile([P, T], U32, name="xw", align_bytes=ALIGN)
+        xs = shared.tile([P, T], U8, name="xs", align_bytes=ALIGN, offset=3840)
+        w1_raw = shared.tile([P, PACK, H], F32, name="w1_raw", align_bytes=ALIGN, offset=29952)
 
         nc.scalar.dma_start(xs[112:P, :].bitcast(I32), x_scales[0].bitcast(I32))
         nc.sync.dma_start(offs_sb[:], offs)
@@ -43,17 +44,17 @@ def tile_picked_pagemix_none_p_kernel(tc, x_words, x_scales, w1, mem, w2, offs, 
         nc.sync.dma_start(slot_sb[:], slot)
 
         nc.vector.memset(xs[0:112, :].bitcast(I32), 0)
-        picked = keep.tile([P, S], U8, name="picked", align_bytes=64)
+        picked = keep.tile([P, S], U8, name="picked", align_bytes=ALIGN)
         on_vector(picked[:], xs[:].indirect(offs_sb[:]))
-        gs = shared.tile([P, S], U8, name="gs", align_bytes=64, offset=8704)
+        gs = shared.tile([P, S], U8, name="gs", align_bytes=ALIGN, offset=4352)
         for q in range(4):
             nc.sync.dma_start(gs[32 * q:32 * q + 4, :].bitcast(I32), picked[112 + 4 * q:116 + 4 * q, :].bitcast(I32))
 
         mem_rows = mem.rearrange("(p t) w -> t p w", t=PACK)
-        page1 = shared.tile([P, U], F32, name="page1", tag="page1", align_bytes=64, offset=4096)
+        page1 = shared.tile([P, U], F32, name="page1", align_bytes=ALIGN, offset=0)
         nc.sync.dma_start(page1[:], mem_rows[1])
-        page3 = shared.tile([P, U], F32, name="page3", tag="page3", align_bytes=64, offset=10112)
-        nc.sync.dma_start(page3[:], mem_rows[3])
+        z = shared.tile([P, PACK * U], F32, name="z", align_bytes=ALIGN, offset=5632)
+        nc.sync.dma_start(z[:, 0:U], mem_rows[0])
 
         w1_src = w1_raw[:].rearrange("p j (m t) -> p m j t", t=PACK)
         w1_codes = {}
@@ -68,130 +69,95 @@ def tile_picked_pagemix_none_p_kernel(tc, x_words, x_scales, w1, mem, w2, offs, 
                 w1_codes[t0 + 2 * i] = codes[:, i * P:(i + 1) * P]
                 w1_scales[t0 + 2 * i] = scales[:, i * P:(i + 1) * P]
 
-        page23 = shared.tile([P, 2 * U], F32, name="page23", align_bytes=64, offset=14336)
-        page01 = shared.tile([P, 2 * U], F32, name="page01", align_bytes=64, offset=22528)
-        w2_rows = w2.rearrange("(p j) c -> p j c", j=PACK)
-        w2_raw = [page[:, U:2 * U].rearrange("p (j c) -> p j c", j=PACK) for page in (page23, page01)]
-        for h, (page, t) in enumerate(((page23, 2), (page01, 0))):
-            nc.sync.dma_start(w2_raw[h], w2_rows[:, :, h * N // 2:(h + 1) * N // 2])
-            nc.sync.dma_start(page[:, 0:U], mem_rows[t])
+        page3 = shared.tile([P, U], F32, name="page3", align_bytes=ALIGN, offset=34304)
+        nc.sync.dma_start(page3[:], mem_rows[3])
+        page2 = shared.tile([P, U], F32, name="page2", align_bytes=ALIGN, offset=30208)
+        nc.sync.dma_start(page2[:], mem_rows[2])
+        w2_raw = shared.tile([P, PACK, N], F32, name="w2_raw", align_bytes=ALIGN, offset=22016)
+        nc.sync.dma_start(w2_raw[:], w2.rearrange("(p j) c -> p j c", j=PACK))
 
         gw = keep.tile([P, S], U32, name="gw", align_bytes=64)
-        for lo, hi in ((0, FIRST), (FIRST, S)):
+        for lo, hi in ((0, HALF), (HALF, S)):
             on_vector(gw[:, lo:hi], xw[:].indirect(offs_sb[:, lo // 16:hi // 16]))
 
         def bank(b):
             return psum.tile([P, BANK], F32, name="bank%d" % b, tag="bank%d" % b)
 
-        pieces = [(1, ((0, P), (P, FIRST))), (3, ((0, P), (P, P + HALF), (P + HALF, S))), (2, ((0, S),)), (0, ((0, S),)), (1, ((FIRST, FIRST + HALF, S),))]
-        ys = {}
-        used = []
-        for t, groups in pieces:
-            first, last = groups[0][0], groups[-1][-1]
-            y = keep.tile([P, last - first], F32, name="y%d_%d" % (t, first), tag="y%d_%d" % (t, first), align_bytes=64)
-            for cuts in groups:
-                acc = bank(len(used))
-                used.append(t)
-                for lo, hi in zip(cuts, cuts[1:]):
-                    nc.tensor.matmul_mx(out=acc[:, lo - cuts[0]:hi - cuts[0]], lhsT=w1_codes[t].bitcast(FP8X4), lhsT_scale=w1_scales[t],
-                                        rhs=gw[:, lo:hi].bitcast(FP8X4), rhs_scale=gs[:, lo:hi], start=True, stop=True)
-                on_scalar(y[:, cuts[0] - first:cuts[-1] - first], acc[:, 0:cuts[-1] - cuts[0]])
-            ys[t, first, last] = y
+        ys = [keep.tile([P, S], F32, name="y%d" % t, align_bytes=64) for t in range(PACK)]
+        pieces = [(1, 0, HALF), (0, 0, HALF), (1, HALF, S), (0, HALF, S), (3, 0, S), (2, 0, S)]
+        for b, (t, lo, hi) in enumerate(pieces):
+            acc = bank(b)
+            nc.tensor.matmul_mx(out=acc[:, 0:hi - lo], lhsT=w1_codes[t].bitcast(FP8X4), lhsT_scale=w1_scales[t],
+                                rhs=gw[:, lo:hi].bitcast(FP8X4), rhs_scale=gs[:, lo:hi], start=True, stop=True)
+            on_scalar(ys[t][:, lo:hi], acc[:, 0:hi - lo])
 
-        def scatter(window, t, lo, hi):
-            on_vector(window[:].indirect(slot_sb[:, lo // 16:hi // 16]), ys[t, lo, hi][:])
-
-        w2_grouped = []
-
-        def round_w2(h):
-            w2_grouped.append(shared.tile([P, N // 2, PACK], BF16, name="w2_grouped%d" % h, tag=("w2_grouped0", "page3")[h], align_bytes=64, offset=(30720, 10112)[h]))
-            on_scalar(w2_grouped[h][:].rearrange("p (c i) j -> p c j i", i=4), w2_raw[h].rearrange("p j (c i) -> p c j i", i=4))
-
-        scatter(page1, 1, 0, FIRST)
-        scatter(page3, 3, 0, S)
-        scatter(page1, 1, FIRST, S)
-        round_w2(0)
-        on_scalar(page23[:, U:2 * U], page3[:])
-        round_w2(1)
-        scatter(page23, 2, 0, S)
-        on_scalar(page01[:, U:2 * U], page1[:])
-
-        starts = [sum(CHUNKS[:i]) for i in range(len(CHUNKS))]
-        z_grouped = [shared.tile([P, cw, PACK], BF16, name="z_grouped%d" % i, align_bytes=64, offset=(4160, 5184, 6208, 7488, 64)[i]) for i, cw in enumerate(CHUNKS)]
-        src23 = page23[:].rearrange("p (h w) -> p w h", h=2)
-        src01 = page01[:].rearrange("p (h w) -> p w h", h=2)
-        for i, cw in enumerate(CHUNKS):
-            on_scalar(z_grouped[i][:, :, 2:4], src23[:, starts[i]:starts[i] + cw, :])
-        scatter(page01, 0, 0, S)
+        on_vector(page1[:].indirect(slot_sb[:]), ys[1][:])
+        nc.scalar.activation(z[:].indirect(slot_sb[:]), ys[0][:], COPY)
+        on_vector(page3[:].indirect(slot_sb[:]), ys[3][:])
+        nc.scalar.activation(page2[:].indirect(slot_sb[:]), ys[2][:], COPY)
+        nc.sync.dma_start(z[:, U:2 * U], page1[:])
+        on_vector(z[:, 3 * U:3 * U + HEAD], page3[:, 0:HEAD])
+        nc.sync.dma_start(z[:, 3 * U + HEAD:4 * U], page3[:, HEAD:U])
 
         w2_codes = {}
         w2_scales = {}
-        w2_half = {}
-
-        def quantize_w2(h):
-            if h == 0:
-                codes = keep.tile([P, 2 * P], U32, name="w2_codes0", align_bytes=64)
-                scales = shared.tile([P, 2 * P], U8, name="w2_scales0", align_bytes=64, offset=7232)
-            else:
-                codes = keep.tile([P, 2 * P], U32, name="w2_codes1", tag="y0_0", align_bytes=64)
-                scales = keep.tile([P, 2 * P], U8, name="w2_scales1", align_bytes=64)
+        w2_grouped = []
+        for h in range(2):
+            grouped = keep.tile([P, N // 2, PACK], BF16, name="w2_grouped%d" % h, align_bytes=64)
+            on_vector(grouped[:].rearrange("p (c i) j -> p c j i", i=4), w2_raw[:, :, h * N // 2:(h + 1) * N // 2].rearrange("p j (c i) -> p c j i", i=4))
+            w2_grouped.append(grouped)
+        for h in range(2):
+            codes = keep.tile([P, 2 * P], U32, name="w2_codes%d" % h, align_bytes=64)
+            scales = keep.tile([P, 2 * P], U8, name="w2_scales%d" % h, align_bytes=64)
             nc.vector.quantize_mx(out=codes[:].bitcast(FP8X4), scales=scales[:], in_=w2_grouped[h][:].rearrange("p c j -> p (c j)"))
-            w2_half[h] = codes, scales
             for i in range(2):
                 w2_codes[2 * h + i] = codes[:, i * P:(i + 1) * P]
                 w2_scales[2 * h + i] = scales[:, i * P:(i + 1) * P]
 
+        starts = [sum(CHUNKS[:i]) for i in range(len(CHUNKS))]
+        for lo, hi in ((0, 128), (128, 256), (256, 512), (512, U)):
+            on_scalar(z[:, 2 * U + lo:2 * U + hi], page2[:, lo:hi])
+
+        z_planes = z[:].rearrange("p (t w) -> p t w", t=PACK)
+        z_grouped = [keep.tile([P, cw, PACK], BF16, name="z_grouped%d" % i, align_bytes=64) for i, cw in enumerate(CHUNKS)]
         z_codes = keep.tile([P, U], U32, name="z_codes", align_bytes=64)
         z_scales = keep.tile([P, U], U8, name="z_scales", align_bytes=64)
 
-        def convert(copy, i, lo, hi):
-            copy(z_grouped[i][:, lo - starts[i]:hi - starts[i], 0:2], src01[:, lo:hi, :])
+        def convert(i):
+            cols = slice(starts[i], starts[i] + CHUNKS[i])
+            on_vector(z_grouped[i][:], z_planes[:, :, cols].rearrange("p t w -> p w t"))
 
         def quantize(i):
             cols = slice(starts[i], starts[i] + CHUNKS[i])
             nc.vector.quantize_mx(out=z_codes[:, cols].bitcast(FP8X4), scales=z_scales[:, cols], in_=z_grouped[i][:].rearrange("p w j -> p (w j)"))
 
-        convert(on_scalar, 4, SPLIT, U)
-        quantize_w2(0)
-        convert(on_vector, 0, 0, 128)
-        convert(on_vector, 1, 128, 256)
-        convert(on_vector, 2, 256, 384)
-        quantize(0)
-        quantize(1)
-        convert(on_vector, 3, 384, 512)
-        quantize(2)
-        convert(on_vector, 4, 512, SPLIT)
-        quantize(3)
-        quantize_w2(1)
-        quantize(4)
+        convert(0)
+        for i in range(1, len(CHUNKS)):
+            convert(i)
+            quantize(i - 1)
+        quantize(len(CHUNKS) - 1)
 
         out_rows = out.rearrange("(a p) w -> p a w", p=P)
+        banks = []
 
-        def multiply(copy, res, a, cuts, b):
-            acc = bank(b)
-            for lo, hi in zip(cuts, cuts[1:]):
-                nc.tensor.matmul_mx(out=acc[:, lo - cuts[0]:hi - cuts[0]], lhsT=w2_codes[a].bitcast(FP8X4), lhsT_scale=w2_scales[a],
-                                    rhs=z_codes[:, lo:hi].bitcast(FP8X4), rhs_scale=z_scales[:, lo:hi], start=True, stop=True)
-            copy(res, acc[:, 0:cuts[-1] - cuts[0]])
+        def store(i, tiles, copies):
+            lo, cw = starts[i], CHUNKS[i]
+            res = keep.tile([P, len(tiles), cw], F32, name="res%d_%d" % (i, tiles[0]), align_bytes=ALIGN)
+            each = len(tiles) // len(copies)
+            for n, copy in enumerate(copies):
+                acc = bank(len(banks) % 8)
+                banks.append(n)
+                for j in range(each):
+                    a = tiles[n * each + j]
+                    nc.tensor.matmul_mx(out=acc[:, j * cw:(j + 1) * cw], lhsT=w2_codes[a].bitcast(FP8X4), lhsT_scale=w2_scales[a],
+                                        rhs=z_codes[:, lo:lo + cw].bitcast(FP8X4), rhs_scale=z_scales[:, lo:lo + cw], start=True, stop=True)
+                copy(res[:, n * each:(n + 1) * each, :].rearrange("p a w -> p (a w)"), acc[:, 0:each * cw])
+            nc.sync.dma_start(out_rows[:, tiles[0]:tiles[-1] + 1, lo:lo + cw], res[:])
 
-        def store(parts):
-            a0, a1 = parts[0][1], parts[-1][1] + 1
-            lo, hi = parts[0][2][0], parts[-1][2][-1]
-            res = keep.tile([P, a1 - a0, hi - lo], F32, name="res%d_%d" % (a0, lo), align_bytes=64)
-            for copy, a, cuts, b in parts:
-                multiply(copy, res[:, a - a0, cuts[0] - lo:cuts[-1] - lo], a, cuts, b)
-            nc.sync.dma_start(out_rows[:, a0:a1, lo:hi], res[:])
-
-        idle = bank(5)
-        for i in range(2):
-            nc.tensor.matmul_mx(out=idle[:, i * 2 * P:(i + 1) * 2 * P], lhsT=w2_codes[i].bitcast(FP8X4), lhsT_scale=w2_scales[i],
-                                rhs=w2_half[0][0][:].bitcast(FP8X4), rhs_scale=w2_half[0][1][:], start=True, stop=True)
-
-        store([(on_scalar, 0, (0, 128), 6), (on_scalar, 0, (128, 256), 0)])
-        store([(on_scalar, 1, (0, 256), 1)])
-        store([(on_scalar, 0, (256, 384), 2), (on_scalar, 0, (384, 512), 3)])
-        store([(on_scalar, 1, (256, 384, 512), 4)])
-        store([(on_scalar, 2, (0, 256), 7), (on_scalar, 2, (256, 384), 5), (on_vector, 2, (384, 512), 6)])
-        store([(on_scalar, 3, (0, 256), 0), (on_vector, 3, (256, 512), 1)])
-        store([(on_scalar, 0, (512, 768), 2), (on_vector, 0, (768, U), 3), (on_scalar, 1, (512, 768), 4), (on_vector, 1, (768, U), 7)])
-        store([(on_scalar, 2, (512, U), 5), (on_vector, 3, (512, U), 0)])
+        store(0, (0, 1, 2, 3), (on_scalar, on_scalar))
+        store(1, (0, 1, 2, 3), (on_scalar, on_scalar))
+        for i in (2, 3):
+            store(i, (0, 1), (on_scalar,))
+            store(i, (2, 3), (on_scalar,))
+        store(4, (0, 1), (on_scalar, on_vector))
+        store(4, (2, 3), (on_scalar, on_vector))

@@ -59,20 +59,20 @@ def tile_picked_pagemix_none_p_kernel(tc, x_words, x_scales, w1, mem, w2, offs, 
         w1_src = w1_raw[:].rearrange("p j (m t) -> p m j t", t=PACK)
         w1_codes = {}
         w1_scales = {}
-        for t0, copy in ((1, on_vector), (0, on_scalar)):
+        for t0, copy in ((0, on_vector), (2, on_scalar)):
             grouped = keep.tile([P, 2, P, PACK], BF16, name="w1_grouped%d" % t0, align_bytes=64)
-            copy(grouped[:].rearrange("p t m j -> p m j t"), w1_src[:, :, :, t0:PACK:2])
+            copy(grouped[:].rearrange("p t m j -> p m j t"), w1_src[:, :, :, t0:t0 + 2])
             codes = keep.tile([P, 2 * P], U32, name="w1_codes%d" % t0, align_bytes=64)
             scales = keep.tile([P, 2 * P], U8, name="w1_scales%d" % t0, align_bytes=64)
             nc.vector.quantize_mx(out=codes[:].bitcast(FP8X4), scales=scales[:], in_=grouped[:].rearrange("p t m j -> p (t m j)"))
             for i in range(2):
-                w1_codes[t0 + 2 * i] = codes[:, i * P:(i + 1) * P]
-                w1_scales[t0 + 2 * i] = scales[:, i * P:(i + 1) * P]
+                w1_codes[t0 + i] = codes[:, i * P:(i + 1) * P]
+                w1_scales[t0 + i] = scales[:, i * P:(i + 1) * P]
 
-        page3 = shared.tile([P, U], F32, name="page3", align_bytes=ALIGN, offset=34304)
-        nc.sync.dma_start(page3[:], mem_rows[3])
-        page2 = shared.tile([P, U], F32, name="page2", align_bytes=ALIGN, offset=30208)
+        page2 = shared.tile([P, U], F32, name="page2", align_bytes=ALIGN, offset=34304)
         nc.sync.dma_start(page2[:], mem_rows[2])
+        page3 = shared.tile([P, U], F32, name="page3", align_bytes=ALIGN, offset=30208)
+        nc.sync.dma_start(page3[:], mem_rows[3])
         w2_raw = shared.tile([P, PACK, N], F32, name="w2_raw", align_bytes=ALIGN, offset=22016)
         nc.sync.dma_start(w2_raw[:], w2.rearrange("(p j) c -> p j c", j=PACK))
 
@@ -84,29 +84,30 @@ def tile_picked_pagemix_none_p_kernel(tc, x_words, x_scales, w1, mem, w2, offs, 
             return psum.tile([P, BANK], F32, name="bank%d" % b, tag="bank%d" % b)
 
         ys = [keep.tile([P, S], F32, name="y%d" % t, align_bytes=64) for t in range(PACK)]
-        pieces = [(1, 0, HALF), (0, 0, HALF), (1, HALF, S), (0, HALF, S), (3, 0, S), (2, 0, S)]
-        for b, (t, lo, hi) in enumerate(pieces):
+        pieces = [(1, 0, HALF, on_vector), (0, 0, HALF, on_scalar), (1, HALF, S, on_scalar), (0, HALF, S, on_scalar), (2, 0, S, on_scalar), (3, 0, S, on_scalar)]
+        for b, (t, lo, hi, copy) in enumerate(pieces):
             acc = bank(b)
             nc.tensor.matmul_mx(out=acc[:, 0:hi - lo], lhsT=w1_codes[t].bitcast(FP8X4), lhsT_scale=w1_scales[t],
                                 rhs=gw[:, lo:hi].bitcast(FP8X4), rhs_scale=gs[:, lo:hi], start=True, stop=True)
-            on_scalar(ys[t][:, lo:hi], acc[:, 0:hi - lo])
+            copy(ys[t][:, lo:hi], acc[:, 0:hi - lo])
 
         on_vector(page1[:].indirect(slot_sb[:]), ys[1][:])
         nc.scalar.activation(z[:].indirect(slot_sb[:]), ys[0][:], COPY)
-        on_vector(page3[:].indirect(slot_sb[:]), ys[3][:])
-        nc.scalar.activation(page2[:].indirect(slot_sb[:]), ys[2][:], COPY)
+        on_vector(page2[:].indirect(slot_sb[:]), ys[2][:])
+        nc.scalar.activation(page3[:].indirect(slot_sb[:]), ys[3][:], COPY)
         nc.sync.dma_start(z[:, U:2 * U], page1[:])
-        on_vector(z[:, 3 * U:3 * U + HEAD], page3[:, 0:HEAD])
-        nc.sync.dma_start(z[:, 3 * U + HEAD:4 * U], page3[:, HEAD:U])
+        on_vector(z[:, 2 * U:2 * U + HEAD], page2[:, 0:HEAD])
+        nc.sync.dma_start(z[:, 2 * U + HEAD:3 * U], page2[:, HEAD:U])
 
         w2_codes = {}
         w2_scales = {}
         w2_grouped = []
         for h in range(2):
-            grouped = keep.tile([P, N // 2, PACK], BF16, name="w2_grouped%d" % h, align_bytes=64)
+            grouped = shared.tile([P, N // 2, PACK], BF16, name="w2_grouped%d" % h, align_bytes=ALIGN, offset=38400 + 2048 * h)
             on_vector(grouped[:].rearrange("p (c i) j -> p c j i", i=4), w2_raw[:, :, h * N // 2:(h + 1) * N // 2].rearrange("p j (c i) -> p c j i", i=4))
             w2_grouped.append(grouped)
-        for h in range(2):
+
+        def quantize_w2(h):
             codes = keep.tile([P, 2 * P], U32, name="w2_codes%d" % h, align_bytes=64)
             scales = keep.tile([P, 2 * P], U8, name="w2_scales%d" % h, align_bytes=64)
             nc.vector.quantize_mx(out=codes[:].bitcast(FP8X4), scales=scales[:], in_=w2_grouped[h][:].rearrange("p c j -> p (c j)"))
@@ -116,48 +117,63 @@ def tile_picked_pagemix_none_p_kernel(tc, x_words, x_scales, w1, mem, w2, offs, 
 
         starts = [sum(CHUNKS[:i]) for i in range(len(CHUNKS))]
         for lo, hi in ((0, 128), (128, 256), (256, 512), (512, U)):
-            on_scalar(z[:, 2 * U + lo:2 * U + hi], page2[:, lo:hi])
+            on_scalar(z[:, 3 * U + lo:3 * U + hi], page3[:, lo:hi])
 
         z_planes = z[:].rearrange("p (t w) -> p t w", t=PACK)
-        z_grouped = [keep.tile([P, cw, PACK], BF16, name="z_grouped%d" % i, align_bytes=64) for i, cw in enumerate(CHUNKS)]
+        z_grouped = {}
         z_codes = keep.tile([P, U], U32, name="z_codes", align_bytes=64)
         z_scales = keep.tile([P, U], U8, name="z_scales", align_bytes=64)
 
         def convert(i):
-            cols = slice(starts[i], starts[i] + CHUNKS[i])
-            on_vector(z_grouped[i][:], z_planes[:, :, cols].rearrange("p t w -> p w t"))
+            lo, cw = starts[i], CHUNKS[i]
+            src = z_planes[:, :, lo:lo + cw]
+            if lo < HEAD:
+                z_grouped[i] = shared.tile([P, cw, PACK], BF16, name="z_grouped%d" % i, align_bytes=ALIGN, offset=38400 + 8 * lo)
+                on_vector(z_grouped[i][:], src.rearrange("p t w -> p w t"))
+            else:
+                z_grouped[i] = shared.tile([P, cw, PACK], BF16, name="z_grouped%d" % i, align_bytes=ALIGN, offset=22016 + 8 * (lo - HEAD))
+                on_vector(z_grouped[i][:].rearrange("p (c i) t -> p c t i", i=4), src.rearrange("p t (c i) -> p c t i", i=4))
 
         def quantize(i):
             cols = slice(starts[i], starts[i] + CHUNKS[i])
             nc.vector.quantize_mx(out=z_codes[:, cols].bitcast(FP8X4), scales=z_scales[:, cols], in_=z_grouped[i][:].rearrange("p w j -> p (w j)"))
 
+        quantize_w2(0)
         convert(0)
-        for i in range(1, len(CHUNKS)):
+        convert(1)
+        quantize(0)
+        quantize(1)
+        quantize_w2(1)
+        for i in range(2, len(CHUNKS)):
             convert(i)
-            quantize(i - 1)
-        quantize(len(CHUNKS) - 1)
+            quantize(i)
 
         out_rows = out.rearrange("(a p) w -> p a w", p=P)
         banks = []
 
-        def store(i, tiles, copies):
-            lo, cw = starts[i], CHUNKS[i]
-            res = keep.tile([P, len(tiles), cw], F32, name="res%d_%d" % (i, tiles[0]), align_bytes=ALIGN)
-            each = len(tiles) // len(copies)
-            for n, copy in enumerate(copies):
-                acc = bank(len(banks) % 8)
-                banks.append(n)
-                for j in range(each):
-                    a = tiles[n * each + j]
-                    nc.tensor.matmul_mx(out=acc[:, j * cw:(j + 1) * cw], lhsT=w2_codes[a].bitcast(FP8X4), lhsT_scale=w2_scales[a],
-                                        rhs=z_codes[:, lo:lo + cw].bitcast(FP8X4), rhs_scale=z_scales[:, lo:lo + cw], start=True, stop=True)
-                copy(res[:, n * each:(n + 1) * each, :].rearrange("p a w -> p (a w)"), acc[:, 0:each * cw])
-            nc.sync.dma_start(out_rows[:, tiles[0]:tiles[-1] + 1, lo:lo + cw], res[:])
+        def store(lo, cw, a0, units):
+            tiles = sorted(set(a for copy, group in units for a, c0, c1 in group))
+            res = keep.tile([P, len(tiles), cw], F32, name="res%d_%d" % (lo, a0), align_bytes=ALIGN)
+            flat = res[:].rearrange("p a w -> p (a w)")
+            done = 0
+            for copy, group in units:
+                acc = bank((6 + len(banks)) % 8)
+                banks.append(copy)
+                at = 0
+                for a, c0, c1 in group:
+                    nc.tensor.matmul_mx(out=acc[:, at:at + c1 - c0], lhsT=w2_codes[a].bitcast(FP8X4), lhsT_scale=w2_scales[a],
+                                        rhs=z_codes[:, c0:c1].bitcast(FP8X4), rhs_scale=z_scales[:, c0:c1], start=True, stop=True)
+                    at = at + c1 - c0
+                copy(flat[:, done:done + at], acc[:, 0:at])
+                done = done + at
+            nc.sync.dma_start(out_rows[:, a0:a0 + len(tiles), lo:lo + cw], res[:])
 
-        store(0, (0, 1, 2, 3), (on_scalar, on_scalar))
-        store(1, (0, 1, 2, 3), (on_scalar, on_scalar))
-        for i in (2, 3):
-            store(i, (0, 1), (on_scalar,))
-            store(i, (2, 3), (on_scalar,))
-        store(4, (0, 1), (on_scalar, on_vector))
-        store(4, (2, 3), (on_scalar, on_vector))
+        store(0, 256, 0, [(on_scalar, [(0, 0, 128)]), (on_scalar, [(0, 128, 256)])])
+        store(0, 256, 1, [(on_scalar, [(1, 0, 256)])])
+        store(0, 256, 2, [(on_scalar, [(2, 0, 256)]), (on_scalar, [(3, 0, 256)])])
+        store(256, 256, 0, [(on_scalar, [(0, 256, 512)]), (on_scalar, [(1, 256, 512)])])
+        store(256, 256, 2, [(on_scalar, [(2, 256, 512), (3, 256, 512)])])
+        store(512, 256, 0, [(on_scalar, [(0, 512, 768), (1, 512, 768)])])
+        store(512, 256, 2, [(on_scalar, [(2, 512, 768)]), (on_vector, [(3, 512, 768)])])
+        store(768, 256, 0, [(on_scalar, [(0, 768, U)]), (on_vector, [(1, 768, U)])])
+        store(768, 256, 2, [(on_scalar, [(2, 768, U)]), (on_vector, [(3, 768, U)])])

@@ -33,9 +33,9 @@ def tile_picked_pagemix_none_p_kernel(tc, x_words, x_scales, w1, mem, w2, offs, 
 
         offs_sb = keep.tile([P, S // 16], U16, name="offs_sb")
         slot_sb = keep.tile([P, S // 16], U16, name="slot_sb")
-        xw = keep.tile([P, T], U32, name="xw", align_bytes=ALIGN)
+        xw = shared.tile([P, T], U32, name="xw", align_bytes=ALIGN, offset=47104)
         xs = shared.tile([P, T], U8, name="xs", align_bytes=ALIGN, offset=3840)
-        w1_raw = shared.tile([P, PACK, H], F32, name="w1_raw", align_bytes=ALIGN, offset=29952)
+        w1_raw = shared.tile([P, PACK, H], F32, name="w1_raw", align_bytes=ALIGN, offset=25856)
 
         nc.scalar.dma_start(xs[112:P, :].bitcast(I32), x_scales[0].bitcast(I32))
         nc.sync.dma_start(offs_sb[:], offs)
@@ -60,21 +60,23 @@ def tile_picked_pagemix_none_p_kernel(tc, x_words, x_scales, w1, mem, w2, offs, 
         w1_codes = {}
         w1_scales = {}
         for t0, copy in ((0, on_vector), (2, on_scalar)):
-            grouped = keep.tile([P, 2, P, PACK], BF16, name="w1_grouped%d" % t0, align_bytes=64)
+            grouped = shared.tile([P, 2, P, PACK], BF16, name="w1_grouped%d" % t0, align_bytes=ALIGN, offset=34304 + 1024 * t0)
             copy(grouped[:].rearrange("p t m j -> p m j t"), w1_src[:, :, :, t0:t0 + 2])
-            codes = keep.tile([P, 2 * P], U32, name="w1_codes%d" % t0, align_bytes=64)
+            codes = shared.tile([P, 2 * P], U32, name="w1_codes%d" % t0, align_bytes=ALIGN, offset=55296 + 512 * t0)
             scales = keep.tile([P, 2 * P], U8, name="w1_scales%d" % t0, align_bytes=64)
             nc.vector.quantize_mx(out=codes[:].bitcast(FP8X4), scales=scales[:], in_=grouped[:].rearrange("p t m j -> p (t m j)"))
             for i in range(2):
                 w1_codes[t0 + i] = codes[:, i * P:(i + 1) * P]
                 w1_scales[t0 + i] = scales[:, i * P:(i + 1) * P]
 
-        page2 = shared.tile([P, U], F32, name="page2", align_bytes=ALIGN, offset=34304)
+        page2 = shared.tile([P, U], F32, name="page2", align_bytes=ALIGN, offset=30208)
         nc.sync.dma_start(page2[:], mem_rows[2])
-        page3 = shared.tile([P, U], F32, name="page3", align_bytes=ALIGN, offset=30208)
+        w2_rows = w2.rearrange("(p j) c -> p j c", j=PACK)
+        w2_raw = [shared.tile([P, PACK, N // 2], F32, name="w2_raw%d" % h, align_bytes=ALIGN, offset=(34304, 55296)[h]) for h in range(2)]
+        page3 = shared.tile([P, U], F32, name="page3", align_bytes=ALIGN, offset=47104)
+        nc.sync.dma_start(w2_raw[0][:], w2_rows[:, :, 0:N // 2])
         nc.sync.dma_start(page3[:], mem_rows[3])
-        w2_raw = shared.tile([P, PACK, N], F32, name="w2_raw", align_bytes=ALIGN, offset=22016)
-        nc.sync.dma_start(w2_raw[:], w2.rearrange("(p j) c -> p j c", j=PACK))
+        nc.sync.dma_start(w2_raw[1][:], w2_rows[:, :, N // 2:N])
 
         gw = keep.tile([P, S], U32, name="gw", align_bytes=64)
         for lo, hi in ((0, HALF), (HALF, S)):
@@ -84,31 +86,45 @@ def tile_picked_pagemix_none_p_kernel(tc, x_words, x_scales, w1, mem, w2, offs, 
             return psum.tile([P, BANK], F32, name="bank%d" % b, tag="bank%d" % b)
 
         ys = [keep.tile([P, S], F32, name="y%d" % t, align_bytes=64) for t in range(PACK)]
-        pieces = [(1, 0, HALF, on_vector), (0, 0, HALF, on_scalar), (1, HALF, S, on_scalar), (0, HALF, S, on_scalar), (2, 0, S, on_scalar), (3, 0, S, on_scalar)]
-        for b, (t, lo, hi, copy) in enumerate(pieces):
+
+        def project(b, t, lo, hi, copy):
             acc = bank(b)
             nc.tensor.matmul_mx(out=acc[:, 0:hi - lo], lhsT=w1_codes[t].bitcast(FP8X4), lhsT_scale=w1_scales[t],
                                 rhs=gw[:, lo:hi].bitcast(FP8X4), rhs_scale=gs[:, lo:hi], start=True, stop=True)
             copy(ys[t][:, lo:hi], acc[:, 0:hi - lo])
 
-        on_vector(page1[:].indirect(slot_sb[:]), ys[1][:])
-        nc.scalar.activation(z[:].indirect(slot_sb[:]), ys[0][:], COPY)
-        on_vector(page2[:].indirect(slot_sb[:]), ys[2][:])
-        nc.scalar.activation(page3[:].indirect(slot_sb[:]), ys[3][:], COPY)
-        nc.sync.dma_start(z[:, U:2 * U], page1[:])
-        on_vector(z[:, 2 * U:2 * U + HEAD], page2[:, 0:HEAD])
-        nc.sync.dma_start(z[:, 2 * U + HEAD:3 * U], page2[:, HEAD:U])
+        def scatter_vector(window, t, lo, hi):
+            on_vector(window[:].indirect(slot_sb[:, lo // 16:hi // 16]), ys[t][:, lo:hi])
+
+        def scatter_scalar(window, t, lo, hi):
+            nc.scalar.activation(window[:].indirect(slot_sb[:, lo // 16:hi // 16]), ys[t][:, lo:hi], COPY)
+
+        project(0, 1, 0, HALF, on_scalar)
+        scatter_vector(page1, 1, 0, HALF)
+        project(1, 0, 0, HALF, on_scalar)
+        project(2, 1, HALF, S, on_scalar)
+        scatter_scalar(z, 0, 0, HALF)
+        scatter_vector(page1, 1, HALF, S)
+        project(3, 2, 0, S, on_scalar)
+        project(4, 3, 0, S, on_scalar)
+        project(5, 0, HALF, S, on_scalar)
+        scatter_scalar(z, 0, HALF, S)
+        scatter_vector(page2, 2, 0, S)
+        scatter_scalar(page3, 3, 0, S)
+        nc.sync.dma_start(z[:, U + HEAD:2 * U], page1[:, HEAD:U])
+        on_vector(z[:, 2 * U:3 * U], page2[:])
 
         w2_codes = {}
         w2_scales = {}
         w2_grouped = []
         for h in range(2):
             grouped = shared.tile([P, N // 2, PACK], BF16, name="w2_grouped%d" % h, align_bytes=ALIGN, offset=38400 + 2048 * h)
-            on_vector(grouped[:].rearrange("p (c i) j -> p c j i", i=4), w2_raw[:, :, h * N // 2:(h + 1) * N // 2].rearrange("p j (c i) -> p c j i", i=4))
+            for lo, hi in (((0, 2 * P),), ((0, P), (P, 2 * P)))[h]:
+                nc.gpsimd.tensor_scalar(grouped[:, lo:hi, :], w2_raw[h][:, :, lo:hi].rearrange("p j c -> p c j"), 1.0, 0.0, mybir.AluOpType.mult, mybir.AluOpType.add)
             w2_grouped.append(grouped)
 
         def quantize_w2(h):
-            codes = keep.tile([P, 2 * P], U32, name="w2_codes%d" % h, align_bytes=64)
+            codes = shared.tile([P, 2 * P], U32, name="w2_codes%d" % h, align_bytes=ALIGN, offset=42496 + 1024 * h)
             scales = keep.tile([P, 2 * P], U8, name="w2_scales%d" % h, align_bytes=64)
             nc.vector.quantize_mx(out=codes[:].bitcast(FP8X4), scales=scales[:], in_=w2_grouped[h][:].rearrange("p c j -> p (c j)"))
             for i in range(2):
@@ -116,42 +132,47 @@ def tile_picked_pagemix_none_p_kernel(tc, x_words, x_scales, w1, mem, w2, offs, 
                 w2_scales[2 * h + i] = scales[:, i * P:(i + 1) * P]
 
         starts = [sum(CHUNKS[:i]) for i in range(len(CHUNKS))]
-        for lo, hi in ((0, 128), (128, 256), (256, 512), (512, U)):
+        for lo, hi in ((HEAD, 512), (512, U)):
             on_scalar(z[:, 3 * U + lo:3 * U + hi], page3[:, lo:hi])
 
         z_planes = z[:].rearrange("p (t w) -> p t w", t=PACK)
-        z_grouped = {}
+        z_head = shared.tile([P, HEAD, PACK], BF16, name="z_head", align_bytes=ALIGN, offset=38400 + 1024)
+        z_grouped = {0: z_head[:, 0:P, :], 1: z_head[:, P:HEAD, :]}
         z_codes = keep.tile([P, U], U32, name="z_codes", align_bytes=64)
         z_scales = keep.tile([P, U], U8, name="z_scales", align_bytes=64)
 
         def convert(i):
             lo, cw = starts[i], CHUNKS[i]
-            src = z_planes[:, :, lo:lo + cw]
             if lo < HEAD:
-                z_grouped[i] = shared.tile([P, cw, PACK], BF16, name="z_grouped%d" % i, align_bytes=ALIGN, offset=38400 + 8 * lo)
-                on_vector(z_grouped[i][:], src.rearrange("p t w -> p w t"))
+                on_vector(z_grouped[i][:, :, 3], page3[:, lo:lo + cw])
             else:
-                z_grouped[i] = shared.tile([P, cw, PACK], BF16, name="z_grouped%d" % i, align_bytes=ALIGN, offset=22016 + 8 * (lo - HEAD))
-                on_vector(z_grouped[i][:].rearrange("p (c i) t -> p c t i", i=4), src.rearrange("p t (c i) -> p c t i", i=4))
+                grouped = shared.tile([P, cw, PACK], BF16, name="z_grouped%d" % i, align_bytes=ALIGN, offset=(49152, 51200 - 256, 47104 + 256)[i - 2])
+                z_grouped[i] = grouped[:]
+                on_vector(grouped[:].rearrange("p (c i) t -> p c t i", i=4), z_planes[:, :, lo:lo + cw].rearrange("p t (c i) -> p c t i", i=4))
 
         def quantize(i):
             cols = slice(starts[i], starts[i] + CHUNKS[i])
-            nc.vector.quantize_mx(out=z_codes[:, cols].bitcast(FP8X4), scales=z_scales[:, cols], in_=z_grouped[i][:].rearrange("p w j -> p (w j)"))
+            nc.vector.quantize_mx(out=z_codes[:, cols].bitcast(FP8X4), scales=z_scales[:, cols], in_=z_grouped[i].rearrange("p w j -> p (w j)"))
 
         quantize_w2(0)
+        quantize_w2(1)
+        on_vector(z_head[:, :, 1], page1[:, 0:HEAD])
+        on_vector(z_head[:, :, 0:3:2], z_planes[:, 0:3:2, 0:HEAD].rearrange("p t w -> p w t"))
         convert(0)
         convert(1)
         quantize(0)
         quantize(1)
-        quantize_w2(1)
-        for i in range(2, len(CHUNKS)):
-            convert(i)
-            quantize(i)
+        convert(2)
+        quantize(2)
+        convert(3)
+        convert(4)
+        quantize(3)
+        quantize(4)
 
         out_rows = out.rearrange("(a p) w -> p a w", p=P)
         banks = []
 
-        def store(lo, cw, a0, units):
+        def store(lo, cw, a0, units, queue=nc.sync):
             tiles = sorted(set(a for copy, group in units for a, c0, c1 in group))
             res = keep.tile([P, len(tiles), cw], F32, name="res%d_%d" % (lo, a0), align_bytes=ALIGN)
             flat = res[:].rearrange("p a w -> p (a w)")
@@ -166,14 +187,14 @@ def tile_picked_pagemix_none_p_kernel(tc, x_words, x_scales, w1, mem, w2, offs, 
                     at = at + c1 - c0
                 copy(flat[:, done:done + at], acc[:, 0:at])
                 done = done + at
-            nc.sync.dma_start(out_rows[:, a0:a0 + len(tiles), lo:lo + cw], res[:])
+            queue.dma_start(out_rows[:, a0:a0 + len(tiles), lo:lo + cw], res[:])
 
         store(0, 256, 0, [(on_scalar, [(0, 0, 128)]), (on_scalar, [(0, 128, 256)])])
         store(0, 256, 1, [(on_scalar, [(1, 0, 256)])])
         store(0, 256, 2, [(on_scalar, [(2, 0, 256)]), (on_scalar, [(3, 0, 256)])])
         store(256, 256, 0, [(on_scalar, [(0, 256, 512)]), (on_scalar, [(1, 256, 512)])])
         store(256, 256, 2, [(on_scalar, [(2, 256, 512), (3, 256, 512)])])
-        store(512, 256, 0, [(on_scalar, [(0, 512, 768), (1, 512, 768)])])
+        store(512, 256, 0, [(on_scalar, [(0, 512, 768)]), (on_vector, [(1, 512, 768)])])
         store(512, 256, 2, [(on_scalar, [(2, 512, 768)]), (on_vector, [(3, 512, 768)])])
-        store(768, 256, 0, [(on_scalar, [(0, 768, U)]), (on_vector, [(1, 768, U)])])
-        store(768, 256, 2, [(on_scalar, [(2, 768, U)]), (on_vector, [(3, 768, U)])])
+        store(768, 256, 0, [(on_vector, [(0, 768, U)]), (on_scalar, [(1, 768, U)])], nc.scalar)
+        store(768, 256, 2, [(on_vector, [(2, 768, U)]), (on_scalar, [(3, 768, U)])], nc.scalar)

@@ -18,8 +18,9 @@ P = 128
 PACK = 4
 BANK = 512
 HALF = S // 2
-CHUNKS = (128, 128, 256, 256, 256)
+CHUNKS = (128, 128, 128, 128, 256, 128, 128)
 HEAD = 256
+QUARTER = U // 4
 ALIGN = 256
 
 
@@ -99,20 +100,21 @@ def tile_picked_pagemix_none_p_kernel(tc, x_words, x_scales, w1, mem, w2, offs, 
         def scatter_scalar(window, t, lo, hi):
             nc.scalar.activation(window[:].indirect(slot_sb[:, lo // 16:hi // 16]), ys[t][:, lo:hi], COPY)
 
-        project(0, 1, 0, HALF, on_scalar)
+        project(0, 1, 0, HALF, on_vector)
         scatter_vector(page1, 1, 0, HALF)
         project(1, 0, 0, HALF, on_scalar)
         project(2, 1, HALF, S, on_scalar)
         scatter_scalar(z, 0, 0, HALF)
         scatter_vector(page1, 1, HALF, S)
         project(3, 2, 0, S, on_scalar)
-        project(4, 3, 0, S, on_scalar)
-        project(5, 0, HALF, S, on_scalar)
+        project(4, 0, HALF, S, on_scalar)
         scatter_scalar(z, 0, HALF, S)
+        project(5, 3, 0, S, on_scalar)
         scatter_vector(page2, 2, 0, S)
         scatter_scalar(page3, 3, 0, S)
-        nc.sync.dma_start(z[:, U + HEAD:2 * U], page1[:, HEAD:U])
-        on_vector(z[:, 2 * U:3 * U], page2[:])
+        nc.sync.dma_start(z[:, U:2 * U], page1[:])
+        on_vector(z[:, 2 * U:2 * U + U // 2], page2[:, 0:U // 2])
+        nc.sync.dma_start(z[:, 2 * U + U // 2:3 * U], page2[:, U // 2:U])
 
         w2_codes = {}
         w2_scales = {}
@@ -146,9 +148,12 @@ def tile_picked_pagemix_none_p_kernel(tc, x_words, x_scales, w1, mem, w2, offs, 
             if lo < HEAD:
                 on_vector(z_grouped[i][:, :, 3], page3[:, lo:lo + cw])
             else:
-                grouped = shared.tile([P, cw, PACK], BF16, name="z_grouped%d" % i, align_bytes=ALIGN, offset=(49152, 51200 - 256, 47104 + 256)[i - 2])
+                grouped = shared.tile([P, cw, PACK], BF16, name="z_grouped%d" % i, align_bytes=ALIGN, offset=(50176, 47104, 51200 - 256, 49408, 48128)[i - 2])
                 z_grouped[i] = grouped[:]
-                on_vector(grouped[:].rearrange("p (c i) t -> p c t i", i=4), z_planes[:, :, lo:lo + cw].rearrange("p t (c i) -> p c t i", i=4))
+                if lo < U // 2:
+                    on_vector(grouped[:], z_planes[:, :, lo:lo + cw].rearrange("p t w -> p w t"))
+                else:
+                    on_vector(grouped[:].rearrange("p (c i) t -> p c t i", i=4), z_planes[:, :, lo:lo + cw].rearrange("p t (c i) -> p c t i", i=4))
 
         def quantize(i):
             cols = slice(starts[i], starts[i] + CHUNKS[i])
@@ -156,45 +161,40 @@ def tile_picked_pagemix_none_p_kernel(tc, x_words, x_scales, w1, mem, w2, offs, 
 
         quantize_w2(0)
         quantize_w2(1)
-        on_vector(z_head[:, :, 1], page1[:, 0:HEAD])
-        on_vector(z_head[:, :, 0:3:2], z_planes[:, 0:3:2, 0:HEAD].rearrange("p t w -> p w t"))
-        convert(0)
-        convert(1)
-        quantize(0)
-        quantize(1)
-        convert(2)
-        quantize(2)
-        convert(3)
+        on_vector(z_head[:, :, 0:3], z_planes[:, 0:3, 0:HEAD].rearrange("p t w -> p w t"))
+        for i in (0, 2):
+            convert(i)
+            convert(i + 1)
+            quantize(i)
+            quantize(i + 1)
         convert(4)
-        quantize(3)
+        convert(5)
         quantize(4)
+        convert(6)
+        quantize(5)
+        quantize(6)
 
         out_rows = out.rearrange("(a p) w -> p a w", p=P)
         banks = []
 
-        def store(lo, cw, a0, units, queue=nc.sync):
-            tiles = sorted(set(a for copy, group in units for a, c0, c1 in group))
-            res = keep.tile([P, len(tiles), cw], F32, name="res%d_%d" % (lo, a0), align_bytes=ALIGN)
-            flat = res[:].rearrange("p a w -> p (a w)")
-            done = 0
-            for copy, group in units:
+        def store(lo, a0, count, units, queue=nc.sync):
+            res = keep.tile([P, count, QUARTER], F32, name="res%d_%d" % (lo, a0), align_bytes=ALIGN)
+            for copy, tiles, cuts in units:
                 acc = bank((6 + len(banks)) % 8)
                 banks.append(copy)
-                at = 0
-                for a, c0, c1 in group:
-                    nc.tensor.matmul_mx(out=acc[:, at:at + c1 - c0], lhsT=w2_codes[a].bitcast(FP8X4), lhsT_scale=w2_scales[a],
-                                        rhs=z_codes[:, c0:c1].bitcast(FP8X4), rhs_scale=z_scales[:, c0:c1], start=True, stop=True)
-                    at = at + c1 - c0
-                copy(flat[:, done:done + at], acc[:, 0:at])
-                done = done + at
-            queue.dma_start(out_rows[:, a0:a0 + len(tiles), lo:lo + cw], res[:])
+                width = cuts[-1] - cuts[0]
+                for j, a in enumerate(tiles):
+                    for c0, c1 in zip(cuts, cuts[1:]):
+                        at = j * width + c0 - cuts[0]
+                        nc.tensor.matmul_mx(out=acc[:, at:at + c1 - c0], lhsT=w2_codes[a].bitcast(FP8X4), lhsT_scale=w2_scales[a],
+                                            rhs=z_codes[:, c0:c1].bitcast(FP8X4), rhs_scale=z_scales[:, c0:c1], start=True, stop=True)
+                copy(res[:, tiles[0] - a0:tiles[-1] + 1 - a0, cuts[0] - lo:cuts[-1] - lo], acc[:, 0:len(tiles) * width].rearrange("p (a w) -> p a w", w=width))
+            queue.dma_start(out_rows[:, a0:a0 + count, lo:lo + QUARTER], res[:])
 
-        store(0, 256, 0, [(on_scalar, [(0, 0, 128)]), (on_scalar, [(0, 128, 256)])])
-        store(0, 256, 1, [(on_scalar, [(1, 0, 256)])])
-        store(0, 256, 2, [(on_scalar, [(2, 0, 256)]), (on_scalar, [(3, 0, 256)])])
-        store(256, 256, 0, [(on_scalar, [(0, 256, 512)]), (on_scalar, [(1, 256, 512)])])
-        store(256, 256, 2, [(on_scalar, [(2, 256, 512), (3, 256, 512)])])
-        store(512, 256, 0, [(on_scalar, [(0, 512, 768)]), (on_vector, [(1, 512, 768)])])
-        store(512, 256, 2, [(on_scalar, [(2, 512, 768)]), (on_vector, [(3, 512, 768)])])
-        store(768, 256, 0, [(on_vector, [(0, 768, U)]), (on_scalar, [(1, 768, U)])], nc.scalar)
-        store(768, 256, 2, [(on_vector, [(2, 768, U)]), (on_scalar, [(3, 768, U)])], nc.scalar)
+        store(0, 0, 2, [(on_scalar, (0, 1), (0, 128)), (on_scalar, (0, 1), (128, 256))])
+        store(0, 2, 2, [(on_scalar, (2,), (0, 256)), (on_scalar, (3,), (0, 256))])
+        store(256, 0, 2, [(on_scalar, (0, 1), (256, 384)), (on_scalar, (0, 1), (384, 512))])
+        store(256, 2, 2, [(on_scalar, (2, 3), (256, 512))])
+        store(512, 0, 2, [(on_scalar, (0,), (512, 768)), (on_scalar, (1,), (512, 768))])
+        store(512, 2, 2, [(on_scalar, (2, 3), (512, 768))])
+        store(768, 0, 4, [(on_vector, (0, 1, 2, 3), (768, 896)), (on_vector, (0, 1), (896, U)), (on_scalar, (2, 3), (896, U))], nc.scalar)

@@ -35,7 +35,7 @@ def tile_picked_pagemix_none_p_kernel(tc, x_words, x_scales, w1, mem, w2, offs, 
         offs_sb = keep.tile([P, S // 16], U16, name="offs_sb")
         slot_sb = keep.tile([P, S // 16], U16, name="slot_sb")
         xw = shared.tile([P, T], U32, name="xw", align_bytes=ALIGN, offset=47104)
-        xs = shared.tile([P, T], U8, name="xs", align_bytes=ALIGN, offset=3840)
+        xs = shared.tile([P, T], U8, name="xs", align_bytes=ALIGN, offset=5888)
         w1_raw = shared.tile([P, PACK, H], F32, name="w1_raw", align_bytes=ALIGN, offset=25856)
 
         nc.scalar.dma_start(xs[112:P, :].bitcast(I32), x_scales[0].bitcast(I32))
@@ -47,14 +47,14 @@ def tile_picked_pagemix_none_p_kernel(tc, x_words, x_scales, w1, mem, w2, offs, 
         nc.vector.memset(xs[0:112, :].bitcast(I32), 0)
         picked = keep.tile([P, S], U8, name="picked", align_bytes=ALIGN)
         on_vector(picked[:], xs[:].indirect(offs_sb[:]))
-        gs = shared.tile([P, S], U8, name="gs", align_bytes=ALIGN, offset=4352)
+        gs = shared.tile([P, S], U8, name="gs", align_bytes=ALIGN, offset=6400)
         for q in range(4):
             nc.sync.dma_start(gs[32 * q:32 * q + 4, :].bitcast(I32), picked[112 + 4 * q:116 + 4 * q, :].bitcast(I32))
 
         mem_rows = mem.rearrange("(p t) w -> t p w", t=PACK)
-        page1 = shared.tile([P, U], F32, name="page1", align_bytes=ALIGN, offset=0)
+        page1 = shared.tile([P, U], F32, name="page1", align_bytes=ALIGN, offset=2048)
         nc.sync.dma_start(page1[:], mem_rows[1])
-        z = shared.tile([P, PACK * U], F32, name="z", align_bytes=ALIGN, offset=5632)
+        z = shared.tile([P, PACK * U], F32, name="z", align_bytes=ALIGN, offset=7680)
         nc.sync.dma_start(z[:, 0:U], mem_rows[0])
 
         w1_src = w1_raw[:].rearrange("p j (m t) -> p m j t", t=PACK)
@@ -80,7 +80,7 @@ def tile_picked_pagemix_none_p_kernel(tc, x_words, x_scales, w1, mem, w2, offs, 
         nc.sync.dma_start(w2_raw[1][:], w2_rows[:, :, N // 2:N])
 
         gw = keep.tile([P, S], U32, name="gw", align_bytes=64)
-        for lo, hi in ((0, HALF), (HALF, S)):
+        for lo, hi in ((0, P), (P, HALF), (HALF, S)):
             on_vector(gw[:, lo:hi], xw[:].indirect(offs_sb[:, lo // 16:hi // 16]))
 
         def bank(b):
@@ -88,11 +88,16 @@ def tile_picked_pagemix_none_p_kernel(tc, x_words, x_scales, w1, mem, w2, offs, 
 
         ys = [keep.tile([P, S], F32, name="y%d" % t, align_bytes=64) for t in range(PACK)]
 
-        def project(b, t, lo, hi, copy):
-            acc = bank(b)
-            nc.tensor.matmul_mx(out=acc[:, 0:hi - lo], lhsT=w1_codes[t].bitcast(FP8X4), lhsT_scale=w1_scales[t],
+        accs = {}
+
+        def project(b, t, lo, hi, at=0):
+            if at == 0:
+                accs[b] = bank(b)
+            nc.tensor.matmul_mx(out=accs[b][:, at:at + hi - lo], lhsT=w1_codes[t].bitcast(FP8X4), lhsT_scale=w1_scales[t],
                                 rhs=gw[:, lo:hi].bitcast(FP8X4), rhs_scale=gs[:, lo:hi], start=True, stop=True)
-            copy(ys[t][:, lo:hi], acc[:, 0:hi - lo])
+
+        def empty(b, t, lo, hi, copy):
+            copy(ys[t][:, lo:hi], accs[b][:, 0:hi - lo])
 
         def scatter_vector(window, t, lo, hi):
             on_vector(window[:].indirect(slot_sb[:, lo // 16:hi // 16]), ys[t][:, lo:hi])
@@ -100,27 +105,36 @@ def tile_picked_pagemix_none_p_kernel(tc, x_words, x_scales, w1, mem, w2, offs, 
         def scatter_scalar(window, t, lo, hi):
             nc.scalar.activation(window[:].indirect(slot_sb[:, lo // 16:hi // 16]), ys[t][:, lo:hi], COPY)
 
-        project(0, 1, 0, HALF, on_vector)
+        project(0, 1, 0, P)
+        project(1, 0, 0, P)
+        project(0, 1, P, HALF, P)
+        empty(0, 1, 0, HALF, on_scalar)
         scatter_vector(page1, 1, 0, HALF)
-        project(1, 0, 0, HALF, on_scalar)
-        project(2, 1, HALF, S, on_scalar)
-        scatter_scalar(z, 0, 0, HALF)
+        project(1, 0, P, HALF, P)
+        empty(1, 0, 0, HALF, on_scalar)
+        project(2, 2, 0, HALF)
+        empty(2, 2, 0, HALF, on_scalar)
+        project(3, 1, HALF, S)
+        empty(3, 1, HALF, S, on_scalar)
         scatter_vector(page1, 1, HALF, S)
-        project(3, 2, 0, S, on_scalar)
-        project(4, 0, HALF, S, on_scalar)
-        scatter_scalar(z, 0, HALF, S)
-        project(5, 3, 0, S, on_scalar)
+        project(4, 0, HALF, S)
+        empty(4, 0, HALF, S, on_scalar)
+        project(5, 2, HALF, S)
+        empty(5, 2, HALF, S, on_scalar)
+        project(6, 3, 0, S)
+        empty(6, 3, 0, S, on_scalar)
+        scatter_scalar(z, 0, 0, S)
         scatter_vector(page2, 2, 0, S)
         scatter_scalar(page3, 3, 0, S)
         nc.sync.dma_start(z[:, U:2 * U], page1[:])
-        on_vector(z[:, 2 * U:2 * U + U // 2], page2[:, 0:U // 2])
-        nc.sync.dma_start(z[:, 2 * U + U // 2:3 * U], page2[:, U // 2:U])
+        on_vector(z[:, 2 * U:2 * U + HEAD], page2[:, 0:HEAD])
+        nc.sync.dma_start(z[:, 2 * U + HEAD:3 * U], page2[:, HEAD:U])
 
         w2_codes = {}
         w2_scales = {}
         w2_grouped = []
         for h in range(2):
-            grouped = shared.tile([P, N // 2, PACK], BF16, name="w2_grouped%d" % h, align_bytes=ALIGN, offset=38400 + 2048 * h)
+            grouped = shared.tile([P, N // 2, PACK], BF16, name="w2_grouped%d" % h, align_bytes=ALIGN, offset=(38400, 0)[h])
             for lo, hi in (((0, 2 * P),), ((0, P), (P, 2 * P)))[h]:
                 nc.gpsimd.tensor_scalar(grouped[:, lo:hi, :], w2_raw[h][:, :, lo:hi].rearrange("p j c -> p c j"), 1.0, 0.0, mybir.AluOpType.mult, mybir.AluOpType.add)
             w2_grouped.append(grouped)
@@ -138,7 +152,7 @@ def tile_picked_pagemix_none_p_kernel(tc, x_words, x_scales, w1, mem, w2, offs, 
             on_scalar(z[:, 3 * U + lo:3 * U + hi], page3[:, lo:hi])
 
         z_planes = z[:].rearrange("p (t w) -> p t w", t=PACK)
-        z_head = shared.tile([P, HEAD, PACK], BF16, name="z_head", align_bytes=ALIGN, offset=38400 + 1024)
+        z_head = shared.tile([P, HEAD, PACK], BF16, name="z_head", align_bytes=ALIGN, offset=1024)
         z_grouped = {0: z_head[:, 0:P, :], 1: z_head[:, P:HEAD, :]}
         z_codes = keep.tile([P, U], U32, name="z_codes", align_bytes=64)
         z_scales = keep.tile([P, U], U8, name="z_scales", align_bytes=64)
@@ -148,7 +162,7 @@ def tile_picked_pagemix_none_p_kernel(tc, x_words, x_scales, w1, mem, w2, offs, 
             if lo < HEAD:
                 on_vector(z_grouped[i][:, :, 3], page3[:, lo:lo + cw])
             else:
-                grouped = shared.tile([P, cw, PACK], BF16, name="z_grouped%d" % i, align_bytes=ALIGN, offset=(50176, 47104, 51200 - 256, 49408, 48128)[i - 2])
+                grouped = shared.tile([P, cw, PACK], BF16, name="z_grouped%d" % i, align_bytes=ALIGN, offset=(50176, 47360, 51200 - 256, 49408, 48128)[i - 2])
                 z_grouped[i] = grouped[:]
                 if lo < U // 2:
                     on_vector(grouped[:], z_planes[:, :, lo:lo + cw].rearrange("p t w -> p w t"))
@@ -162,11 +176,14 @@ def tile_picked_pagemix_none_p_kernel(tc, x_words, x_scales, w1, mem, w2, offs, 
         quantize_w2(0)
         quantize_w2(1)
         on_vector(z_head[:, :, 0:3], z_planes[:, 0:3, 0:HEAD].rearrange("p t w -> p w t"))
-        for i in (0, 2):
-            convert(i)
-            convert(i + 1)
-            quantize(i)
-            quantize(i + 1)
+        convert(0)
+        convert(1)
+        quantize(0)
+        quantize(1)
+        convert(2)
+        convert(3)
+        quantize(2)
+        quantize(3)
         convert(4)
         convert(5)
         quantize(4)
@@ -180,7 +197,7 @@ def tile_picked_pagemix_none_p_kernel(tc, x_words, x_scales, w1, mem, w2, offs, 
         def store(lo, a0, count, units, queue=nc.sync):
             res = keep.tile([P, count, QUARTER], F32, name="res%d_%d" % (lo, a0), align_bytes=ALIGN)
             for copy, tiles, cuts in units:
-                acc = bank((6 + len(banks)) % 8)
+                acc = bank((7 + len(banks)) % 8)
                 banks.append(copy)
                 width = cuts[-1] - cuts[0]
                 for j, a in enumerate(tiles):

from contextlib import ExitStack

import concourse.mybir as mybir

K, T, S, H, U, N = 512, 2048, 512, 512, 1024, 512
FLOPS = 2 * K * H * S + 2 * H * N * U

F32 = mybir.dt.float32
BF16 = mybir.dt.bfloat16
I32 = mybir.dt.int32
U32 = mybir.dt.uint32
U16 = mybir.dt.uint16
U8 = mybir.dt.uint8
FP8X4 = mybir.dt.float8_e4m3fn_x4
COPY = mybir.ActivationFunctionType.Copy

P = 128
PACK = 4
BANK = 512
HALF = S // 2
CHUNKS = (128, 128, 128, 128, 256, 128, 128)
HEAD = 256
QUARTER = U // 4
ALIGN = 256


def tile_picked_pagemix_none_p_kernel(tc, x_words, x_scales, w1, mem, w2, offs, slot, out):
    nc = tc.nc
    on_scalar, on_vector = nc.scalar.copy, nc.vector.tensor_copy
    with ExitStack() as ctx:
        keep = ctx.enter_context(tc.tile_pool(name="keep", bufs=1))
        shared = ctx.enter_context(tc.tile_pool(name="shared", bufs=1))
        psum = ctx.enter_context(tc.psum_pool(name="psum", bufs=1))

        offs_sb = keep.tile([P, S // 16], U16, name="offs_sb")
        slot_sb = keep.tile([P, S // 16], U16, name="slot_sb")
        xw = shared.tile([P, T], U32, name="xw", align_bytes=ALIGN, offset=47104)
        xs = shared.tile([P, T], U8, name="xs", align_bytes=ALIGN, offset=5888)
        w1_raw = shared.tile([P, PACK, H], F32, name="w1_raw", align_bytes=ALIGN, offset=25856)

        nc.scalar.dma_start(xs[112:P, :].bitcast(I32), x_scales[0].bitcast(I32))
        nc.sync.dma_start(offs_sb[:], offs)
        nc.sync.dma_start(w1_raw[:], w1.rearrange("(p j) c -> p j c", j=PACK))
        nc.sync.dma_start(xw[:].bitcast(I32), x_words[0].rearrange("p c r -> p (c r)").bitcast(I32))
        nc.sync.dma_start(slot_sb[:], slot)

        nc.vector.memset(xs[0:112, :].bitcast(I32), 0)
        picked = keep.tile([P, S], U8, name="picked", align_bytes=ALIGN)
        on_vector(picked[:], xs[:].indirect(offs_sb[:]))
        gs = shared.tile([P, S], U8, name="gs", align_bytes=ALIGN, offset=6400)
        for q in range(4):
            nc.sync.dma_start(gs[32 * q:32 * q + 4, :].bitcast(I32), picked[112 + 4 * q:116 + 4 * q, :].bitcast(I32))

        mem_rows = mem.rearrange("(p t) w -> t p w", t=PACK)
        page1 = shared.tile([P, U], F32, name="page1", align_bytes=ALIGN, offset=2048)
        nc.sync.dma_start(page1[:], mem_rows[1])
        z = shared.tile([P, PACK * U], F32, name="z", align_bytes=ALIGN, offset=7680)
        nc.sync.dma_start(z[:, 0:U], mem_rows[0])

        w1_src = w1_raw[:].rearrange("p j (m t) -> p m j t", t=PACK)
        w1_codes = {}
        w1_scales = {}
        for t0, copy in ((0, on_vector), (2, on_scalar)):
            grouped = shared.tile([P, 2, P, PACK], BF16, name="w1_grouped%d" % t0, align_bytes=ALIGN, offset=34304 + 1024 * t0)
            copy(grouped[:].rearrange("p t m j -> p m j t"), w1_src[:, :, :, t0:t0 + 2])
            codes = shared.tile([P, 2 * P], U32, name="w1_codes%d" % t0, align_bytes=ALIGN, offset=55296 + 512 * t0)
            scales = keep.tile([P, 2 * P], U8, name="w1_scales%d" % t0, align_bytes=64)
            nc.vector.quantize_mx(out=codes[:].bitcast(FP8X4), scales=scales[:], in_=grouped[:].rearrange("p t m j -> p (t m j)"))
            for i in range(2):
                w1_codes[t0 + i] = codes[:, i * P:(i + 1) * P]
                w1_scales[t0 + i] = scales[:, i * P:(i + 1) * P]

        page2 = shared.tile([P, U], F32, name="page2", align_bytes=ALIGN, offset=30208)
        nc.sync.dma_start(page2[:], mem_rows[2])
        w2_rows = w2.rearrange("(p j) c -> p j c", j=PACK)
        w2_raw = [shared.tile([P, PACK, N // 2], F32, name="w2_raw%d" % h, align_bytes=ALIGN, offset=(34304, 55296)[h]) for h in range(2)]
        page3 = shared.tile([P, U], F32, name="page3", align_bytes=ALIGN, offset=47104)
        nc.sync.dma_start(w2_raw[0][:], w2_rows[:, :, 0:N // 2])
        nc.sync.dma_start(page3[:], mem_rows[3])
        nc.sync.dma_start(w2_raw[1][:], w2_rows[:, :, N // 2:N])

        gw = keep.tile([P, S], U32, name="gw", align_bytes=64)
        for lo, hi in ((0, P), (P, HALF), (HALF, S)):
            on_vector(gw[:, lo:hi], xw[:].indirect(offs_sb[:, lo // 16:hi // 16]))

        def bank(b):
            return psum.tile([P, BANK], F32, name="bank%d" % b, tag="bank%d" % b)

        ys = [keep.tile([P, S], F32, name="y%d" % t, align_bytes=64) for t in range(PACK)]

        accs = {}

        def project(b, t, lo, hi, at=0):
            if at == 0:
                accs[b] = bank(b)
            nc.tensor.matmul_mx(out=accs[b][:, at:at + hi - lo], lhsT=w1_codes[t].bitcast(FP8X4), lhsT_scale=w1_scales[t],
                                rhs=gw[:, lo:hi].bitcast(FP8X4), rhs_scale=gs[:, lo:hi], start=True, stop=True)

        def empty(b, t, lo, hi, copy):
            copy(ys[t][:, lo:hi], accs[b][:, 0:hi - lo])

        def scatter_vector(window, t, lo, hi):
            on_vector(window[:].indirect(slot_sb[:, lo // 16:hi // 16]), ys[t][:, lo:hi])

        def scatter_scalar(window, t, lo, hi):
            nc.scalar.activation(window[:].indirect(slot_sb[:, lo // 16:hi // 16]), ys[t][:, lo:hi], COPY)

        project(0, 1, 0, P)
        project(1, 0, 0, P)
        project(0, 1, P, HALF, P)
        empty(0, 1, 0, HALF, on_scalar)
        scatter_vector(page1, 1, 0, HALF)
        project(1, 0, P, HALF, P)
        empty(1, 0, 0, HALF, on_scalar)
        project(2, 2, 0, HALF)
        empty(2, 2, 0, HALF, on_scalar)
        project(3, 1, HALF, S)
        empty(3, 1, HALF, S, on_scalar)
        scatter_vector(page1, 1, HALF, S)
        project(4, 0, HALF, S)
        empty(4, 0, HALF, S, on_scalar)
        project(5, 2, HALF, S)
        empty(5, 2, HALF, S, on_scalar)
        project(6, 3, 0, S)
        empty(6, 3, 0, S, on_scalar)
        scatter_scalar(z, 0, 0, S)
        scatter_vector(page2, 2, 0, S)
        scatter_scalar(page3, 3, 0, S)
        nc.sync.dma_start(z[:, U:2 * U], page1[:])
        on_vector(z[:, 2 * U:2 * U + HEAD], page2[:, 0:HEAD])
        nc.sync.dma_start(z[:, 2 * U + HEAD:3 * U], page2[:, HEAD:U])

        w2_codes = {}
        w2_scales = {}
        w2_grouped = []
        for h in range(2):
            grouped = shared.tile([P, N // 2, PACK], BF16, name="w2_grouped%d" % h, align_bytes=ALIGN, offset=(38400, 0)[h])
            for lo, hi in (((0, 2 * P),), ((0, P), (P, 2 * P)))[h]:
                nc.gpsimd.tensor_scalar(grouped[:, lo:hi, :], w2_raw[h][:, :, lo:hi].rearrange("p j c -> p c j"), 1.0, 0.0, mybir.AluOpType.mult, mybir.AluOpType.add)
            w2_grouped.append(grouped)

        def quantize_w2(h):
            codes = shared.tile([P, 2 * P], U32, name="w2_codes%d" % h, align_bytes=ALIGN, offset=42496 + 1024 * h)
            scales = keep.tile([P, 2 * P], U8, name="w2_scales%d" % h, align_bytes=64)
            nc.vector.quantize_mx(out=codes[:].bitcast(FP8X4), scales=scales[:], in_=w2_grouped[h][:].rearrange("p c j -> p (c j)"))
            for i in range(2):
                w2_codes[2 * h + i] = codes[:, i * P:(i + 1) * P]
                w2_scales[2 * h + i] = scales[:, i * P:(i + 1) * P]

        starts = [sum(CHUNKS[:i]) for i in range(len(CHUNKS))]
        for lo, hi in ((HEAD, 512), (512, U)):
            on_scalar(z[:, 3 * U + lo:3 * U + hi], page3[:, lo:hi])

        z_planes = z[:].rearrange("p (t w) -> p t w", t=PACK)
        z_head = shared.tile([P, HEAD, PACK], BF16, name="z_head", align_bytes=ALIGN, offset=1024)
        z_grouped = {0: z_head[:, 0:P, :], 1: z_head[:, P:HEAD, :]}
        z_codes = keep.tile([P, U], U32, name="z_codes", align_bytes=64)
        z_scales = keep.tile([P, U], U8, name="z_scales", align_bytes=64)

        def convert(i):
            lo, cw = starts[i], CHUNKS[i]
            if lo < HEAD:
                on_vector(z_grouped[i][:, :, 3], page3[:, lo:lo + cw])
            else:
                grouped = shared.tile([P, cw, PACK], BF16, name="z_grouped%d" % i, align_bytes=ALIGN, offset=(50176, 47360, 51200 - 256, 49408, 48128)[i - 2])
                z_grouped[i] = grouped[:]
                if lo < U // 2:
                    on_vector(grouped[:], z_planes[:, :, lo:lo + cw].rearrange("p t w -> p w t"))
                else:
                    on_vector(grouped[:].rearrange("p (c i) t -> p c t i", i=4), z_planes[:, :, lo:lo + cw].rearrange("p t (c i) -> p c t i", i=4))

        def quantize(i):
            cols = slice(starts[i], starts[i] + CHUNKS[i])
            nc.vector.quantize_mx(out=z_codes[:, cols].bitcast(FP8X4), scales=z_scales[:, cols], in_=z_grouped[i].rearrange("p w j -> p (w j)"))

        quantize_w2(0)
        quantize_w2(1)
        on_vector(z_head[:, :, 0:3], z_planes[:, 0:3, 0:HEAD].rearrange("p t w -> p w t"))
        convert(0)
        convert(1)
        quantize(0)
        quantize(1)
        convert(2)
        convert(3)
        quantize(2)
        quantize(3)
        convert(4)
        convert(5)
        quantize(4)
        convert(6)
        quantize(5)
        quantize(6)

        out_rows = out.rearrange("(a p) w -> p a w", p=P)
        banks = []

        def store(lo, a0, count, units, queue=nc.sync):
            res = keep.tile([P, count, QUARTER], F32, name="res%d_%d" % (lo, a0), align_bytes=ALIGN)
            for copy, tiles, cuts in units:
                acc = bank((7 + len(banks)) % 8)
                banks.append(copy)
                width = cuts[-1] - cuts[0]
                for j, a in enumerate(tiles):
                    for c0, c1 in zip(cuts, cuts[1:]):
                        at = j * width + c0 - cuts[0]
                        nc.tensor.matmul_mx(out=acc[:, at:at + c1 - c0], lhsT=w2_codes[a].bitcast(FP8X4), lhsT_scale=w2_scales[a],
                                            rhs=z_codes[:, c0:c1].bitcast(FP8X4), rhs_scale=z_scales[:, c0:c1], start=True, stop=True)
                copy(res[:, tiles[0] - a0:tiles[-1] + 1 - a0, cuts[0] - lo:cuts[-1] - lo], acc[:, 0:len(tiles) * width].rearrange("p (a w) -> p a w", w=width))
            queue.dma_start(out_rows[:, a0:a0 + count, lo:lo + QUARTER], res[:])

        store(0, 0, 2, [(on_scalar, (0, 1), (0, 128)), (on_scalar, (0, 1), (128, 256))])
        store(0, 2, 2, [(on_scalar, (2,), (0, 256)), (on_scalar, (3,), (0, 256))])
        store(256, 0, 2, [(on_scalar, (0, 1), (256, 384)), (on_scalar, (0, 1), (384, 512))])
        store(256, 2, 2, [(on_scalar, (2, 3), (256, 512))])
        store(512, 0, 2, [(on_scalar, (0,), (512, 768)), (on_scalar, (1,), (512, 768))])
        store(512, 2, 2, [(on_scalar, (2, 3), (512, 768))])
        store(768, 0, 4, [(on_vector, (0, 1, 2, 3), (768, 896)), (on_vector, (0, 1), (896, U)), (on_scalar, (2, 3), (896, U))], nc.scalar)
